import numpy as np, ml_dtypes
CORES = [23,119,17,113]
N = 4
BF = ml_dtypes.bfloat16
def gentries(a):
    return np.ascontiguousarray(a.reshape(8, 16, -1).transpose(0, 2, 1)).reshape(8, -1)
def gtable(e):
    e = np.asarray(e); return np.ascontiguousarray(e.reshape(8, -1, 16).transpose(0, 2, 1)).reshape(128, -1).astype(np.int32)
V, R, M, RO, P, H, CAP, NEED = 4096, 2048, 3, 3, 6, 2, 256, 9
S, TOP = V // N, 2 ** 20 - 1
def parts(rng):
    base = rng.integers(0, 2 ** 20, (1, 8, 16, 1)); amp = np.exp2(10 + 7 * rng.random((N, 8, 1, R)))
    x = np.clip(base + amp * rng.standard_normal((N, 8, 16, R)), 0, TOP).astype(np.int64)
    t = (np.exp2(14 + 3.5 * rng.random((N, 8, 1, 1))) * (0.5 + rng.random((N, 8, 16, 1)))).astype(np.int64)
    lv = rng.integers(0, V, (N, 8, P, R)); lv = np.where(rng.random((N, 8, 1, R)) < 0.5, np.sort(lv, axis=2), lv)
    cd = rng.integers(0, R, (N, 8, RO, M, V))
    return x, t, lv, cd
def pack(x, t, lv, cd):
    return {"px": np.ascontiguousarray(x.reshape(N, 128, R)).astype(np.int32), "th": np.ascontiguousarray(t.reshape(N, 128, 1)).astype(np.int32),
            "ray": np.stack([gtable(a.reshape(8, -1)) for a in lv]), "cand": np.stack([gtable(a.reshape(8, -1)) for a in cd])}
def setup_inputs(rng):
    return pack(*parts(rng))
def setup_inputs_room(rng):
    x, t, lv, cd = parts(rng); h = R // 8
    t = rng.integers(2 ** 14, 2 ** 15, (N, 8, 16, 1)); x = rng.integers(2 ** 18, 2 ** 19, (1, 8, 16, 1)) + rng.integers(0, 2 ** 13, (N, 8, 16, R))
    inc = np.zeros((8, V), bool); own = np.arange(V) // S
    for o in range(N):
        for g in range(8):
            n = int(rng.choice(np.array([0, 1, CAP - 1, CAP, CAP + 1, S]))); last = o == N - 1 and g < 4
            if o == 0: n = (CAP, CAP + 1, S, CAP - 1, 1, 0, CAP, CAP + 1)[g]
            if last: n = (CAP, 1, CAP - 1, CAP)[g]
            s = rng.permutation(S)[:n]
            if last and not np.any(s == S - 1): s[0] = S - 1
            inc[g, o * S + s] = True
    for a in range(N):
        for g in range(8):
            o = rng.permutation(R); hot, watch, calm = o[:h], o[h:2 * h], o[h:]
            m = np.argsort(rng.random((16, h)), axis=0) < rng.integers(NEED, 17, h)
            x[a, g][:, hot] += m * (rng.choice(np.array([-1, 1]), h) * rng.integers(2 ** 16, 2 ** 17, h))
            lv[a, g, 0, o[:2 * h]] = V - 1; cd[a, g, 0] = rng.choice(calm, (M, V))
            for who, back in ((hot, 1), (watch, 2)):
                v = np.flatnonzero(inc[g] & ((own + back) % N == a))
                cd[a, g, 0, rng.integers(0, M, len(v)), v] = rng.choice(who, len(v))
    return pack(x, t, lv, cd)
def setup_inputs_ties(rng):
    x, t, lv, cd = parts(rng); n = min(R // 8, S)
    base = rng.choice(np.array([0, 2 ** 19, TOP]), 8); base[0] = 0; base[1] = TOP; base[2] = 2 ** 19; sg = np.where(base > 2 ** 19, -1, 1)
    t = rng.choice(np.array([0, 1, 1000, 2 ** 18, 2 ** 19 - 8]), (N, 8, 1, 1)) + rng.integers(0, 3, (N, 8, 16, 1))
    x = np.tile(base.reshape(1, 8, 1, 1), (N, 1, 16, R))
    for a in range(N):
        for g in range(8):
            o = rng.permutation(R); hot, watch, calm = o[:n], o[n:2 * n], o[n:]; b, e = (a - 1) % N, (a - 2) % N
            m = (np.argsort(rng.random((16, n)), axis=0) < rng.choice(np.array([NEED - 1, NEED, 16]), n)).astype(np.int64)
            x[a, g][:, hot] = base[g] + sg[g] * (t[b, g] + m)
            v = b * S + rng.permutation(S)[:n]
            lv[a, g, 0, hot] = np.where(rng.random(n) < 0.4, v, np.where(rng.random(n) < 0.5, V - 1, np.maximum(v - 1, 0)))
            lv[a, g, 0, watch] = V - 1
            cd[a, g, 0] = rng.choice(calm, (M, V)); cd[a, g, 0, 0, v] = hot
            cd[a, g, 0, M - 1, e * S:(e + 1) * S] = rng.choice(watch, S)
    return pack(x, t, lv, cd)
def setup_inputs_alike(rng):
    x, t, lv, cd = parts(rng)
    cd[:, ::4] = rng.choice(np.array([0, R - 1, R // 2, 5]), (N, 2, RO, M, V)); cd[:, 3] = cd[:, 3][:, :, :1]
    lv[:, 1::2] = lv[:, 1::2, :1]
    lv[:, 2] = rng.choice(np.array([0, V - 1]), (N, P, R)); lv[:, 6] = rng.integers(0, 16, (N, P, R))
    return pack(x, t, lv, cd)
def setup_inputs_dim(rng):
    x, t, lv, cd = parts(rng); q = rng.permutation(N); k = int(rng.integers(0, 7)); o = int(q[1])
    lv[:, k] = lv[:, k] // 2; lv[q[0], :7] = rng.integers(0, 4, (7, P, R)); t[o] = TOP; t[q[2]] = 0
    for a, pixel in ((int(q[0]), 0), (int(q[3]), TOP)):
        s = rng.permutation(R)[:R // 16]; x[a, 7][:, s] = pixel; lv[a, 7, 0, s] = V - 1
        cd[a, 7, 0, 0, o * S:(o + 1) * S] = rng.choice(s, S)
    return pack(x, t, lv, cd)
def setup_inputs_spread(rng):
    x, t, lv, cd = parts(rng)
    t = np.minimum(np.exp2(10 + 10 * rng.random((N, 8, 16, 1))).astype(np.int64), TOP)
    x = np.minimum((np.exp2(20 * rng.random((N, 8, 1, R))) * rng.random((N, 8, 16, R))).astype(np.int64), TOP)
    return pack(x, t, lv, cd)
def check_inputs(d):
    bad = []
    for k, lo, hi in (("px", 0, TOP), ("th", 0, TOP), ("ray", 0, V - 1), ("cand", 0, R - 1)):
        if np.min(d[k]) < lo or np.max(d[k]) > hi: bad.append("range of " + k)
    return bad
def reference(px, th, ray, cand):
    x = px.astype(np.int64).reshape(N, 8, 16, R); t = th.astype(np.int64).reshape(N, 8, 16, 1)
    lv = np.stack([gentries(a) for a in ray]).astype(np.int64).reshape(N, 8, P, R)
    cd = np.stack([gentries(a) for a in cand]).astype(np.int64).reshape(N, 8, RO, M, V)
    c = np.zeros((N, 8, R), np.int64); number = np.arange(V)
    for rnd in range(RO):
        w = np.take_along_axis(lv, c[:, :, None, :], 2)[:, :, 0]
        lo = np.full((8, 16, V), TOP + 1, np.int64); hi = np.full((8, 16, V), -1, np.int64)
        for a in range(N):
            for m in range(M):
                ix = cd[a, :, rnd, m]
                sees = (number <= np.take_along_axis(w[a], ix, 1))[:, None, :]
                v = np.take_along_axis(x[a], ix[:, None, :], 2)
                lo = np.minimum(lo, np.where(sees, v, TOP + 1)); hi = np.maximum(hi, np.where(sees, v, -1))
        carved = np.zeros((8, V), bool)
        for o in range(N):
            far = (hi[:, :, o * S:(o + 1) * S] - lo[:, :, o * S:(o + 1) * S] > t[o]).astype(np.int64)
            odd = np.add.reduce(far, axis=1) >= NEED
            carved[:, o * S:(o + 1) * S] = odd & (np.add.accumulate(odd.astype(np.int64), axis=1) <= CAP)
        for step in range(H):
            w = np.take_along_axis(lv, c[:, :, None, :], 2)[:, :, 0]
            nx, nc = [], []
            for a in range(N):
                gone = np.take_along_axis(carved, w[a], 1); e = np.take_along_axis(lo, w[a][:, None, :], 2)
                nx.append(np.where(gone[:, None, :], np.clip(x[a] + ((x[a] - e) >> 2), 0, TOP), x[a]))
                nc.append(np.minimum(c[a] + gone.astype(np.int64), P - 1))
            x = np.stack(nx); c = np.stack(nc)
    yc = np.stack([gtable(c[a]) for a in range(N)])
    return {"yx": x.reshape(N, 128, R).astype(np.float32), "yc": yc.astype(np.float32)}

@@ -1,0 +1,477 @@
+from concourse.bass import DstId, RemoteDMATransfer
+from concourse.mybir import AluOpType as A, ActivationFunctionType as F
+
+TOP = 2 ** 20 - 1
+SCRATCH = {}
+
+
+def _buf(where, dtype, **shapes):
+    for n, s in shapes.items():
+        SCRATCH[n] = (where, s if isinstance(s, list) else [128, s], dtype)
+
+
+_buf("dram", "int32", sp=[4, 128, 512], lp=[4, 128, 512], sr=[4, 128, 192], lr=[4, 128, 192], cr=[4, 32, 3, 4, 3, 64], sc=[12, 128, 192])
+_buf("dram", "float32", so=[16, 128, 128], lo=[16, 128, 128], sy=[4, 128, 32], ly=[4, 128, 32])
+_buf("sbuf", "int32", cg0=768, cg1=768, cg2=768, ca=768, xi=2048, rayi=768, tho=1, thl=4, thi=1,
+     zi=256, it0=144, it1=144, vci=384, pc=1, lane=1, grp=1, oi=1, xi4=4, xj4=4, ish=128, im16=128)
+_buf("sbuf", "uint16", lw0=768, lw1=768, lw2=768, lx=768, ln=256, oe=256)
+_buf("sbuf", "bfloat16", wr=12288, fl=1024, m2=128, mcb=144, mid=128, mb2=144, mbc=128, mex=2048, vct=384)
+_buf("sbuf", "float32", xb0=768, xb1=768, xb2=768, thf=1, xw=8192, wt=8192, mt=4096, et=4104, xg=4096, le=384, l1=192, l2=96,
+     l3=32, lm=384, le2=384, lt=1024, odd=64, zz=64, cu=80, cs=80, cv=64, eg=4096, la=768, lb=768, dd=640, zf=256, f1=128, ft=256, fu=128,
+     cc=128, cf=128, lanef=1, grpf=1, of=1, k0=1, nk0=1, g16=1, nb=2, pb=2, colx=4, cole=1, lmk=16, mbo=128, mgt=128, mtri=128)
+_buf("psum", "float32", pA=2048, pB=1024, pC=512, pD=512)
+PSUM = ("pA", "pB", "pC", "pD")
+ENG = {"v": "q_v", "s": "q_s", "t": "q_t", "g": "q_g"}
+DSEM = ["d%d" % j for j in range(64)]
+SEMAPHORES = list(ENG.values()) + DSEM + ["r_ray", "r_c0", "r_px", "r_th", "r_c1", "r_c2", "r_yc", "r_x0", "r_x1", "r_x2", "r_x3", "r_loc"]
+VSHARE = 3
+CHUNKS = ((0, 1024), (1024, 2048))
+CHUNKS_END = ((0, 512), (512, 1024), (1024, 1536), (1536, 2048))
+
+
+def rank_program(g, core, T, topo):
+    me = T.rank_of(core)
+    if me is None:
+        return
+    Q = {"v": g.vector, "s": g.scalar, "t": g.tensor, "y": g.sync, "g": g}
+    known = {q: {} for q in Q}
+    snap = {}
+    cnt = {q: 0 for q in ENG}
+    hist = {}
+    allsem = {}
+    nd = [0]
+
+    def wait(q, tok):
+        sem, val = tok
+        if known[q].get(sem, 0) >= val:
+            return
+        Q[q].wait_ge(T.sem[sem], val)
+        known[q][sem] = val
+        for s2, v2 in snap.get(tok, {}).items():
+            known[q][s2] = max(known[q].get(s2, 0), v2)
+
+    def waits(q, q0, reads, writes):
+        toks = {}
+        for wr, accs in ((False, reads), (True, writes)):
+            for buf, lo, hi in accs:
+                for (l, h, w, q2, tok) in hist.get(buf, ()):
+                    same = q2 == q0 and q0 != "dma"
+                    if buf in PSUM and not same:
+                        hit = l // 512 <= (hi - 1) // 512 and lo // 512 <= (h - 1) // 512
+                    else:
+                        hit = l < hi and lo < h and (w or wr) and not (same and q0 == "t")
+                    if hit:
+                        toks[tok[0]] = max(toks.get(tok[0], 0), tok[1])
+        for s in sorted(toks):
+            wait(q, (s, toks[s]))
+
+    def note(q, reads, writes, tok):
+        for buf, lo, hi in writes:
+            hist[buf] = [e for e in hist.get(buf, ()) if not (lo <= e[0] and e[1] <= hi)] + [(lo, hi, True, q, tok)]
+        for buf, lo, hi in reads:
+            hist[buf] = [e for e in hist.get(buf, ()) if not (lo <= e[0] and e[1] <= hi and not e[2] and e[3] == q and q in ENG)] + [(lo, hi, False, q, tok)]
+
+    def R(n, a=0, b=None):
+        b = SCRATCH[n][1][-1] if b is None else b
+        return (T[n][:, a:b], [(n, a, b)])
+
+    def ind(win, off):
+        return (win[0].indirect(off[0]), win[1] + off[1])
+
+    def op(q, fn, ins, outs):
+        rd = [r for v in ins if isinstance(v, tuple) for r in v[1]]
+        wr = [r for v in outs for r in v[1]]
+        waits(q, q, rd, wr)
+        i = fn()
+        cnt[q] += 1
+        i.then_inc(T.sem[ENG[q]], 1)
+        tok = (ENG[q], cnt[q])
+        allsem[ENG[q]] = cnt[q]
+        snap[tok] = dict(known[q])
+        note(q, rd, wr, tok)
+
+    def dma(qs, items, ins, outs):
+        sem = DSEM[nd[0]]
+        nd[0] += 1
+        kn = {}
+        for q in qs:
+            waits(q, "dma", ins, outs)
+            for s, v in known[q].items():
+                kn[s] = max(kn.get(s, 0), v)
+        for j, (o, i) in enumerate(items):
+            Q[qs[j % len(qs)]].dma_start(o, i).then_inc(T.sem[sem], 16)
+        tok = (sem, 16 * len(items))
+        allsem[sem] = tok[1]
+        snap[tok] = kn
+        note("dma", ins, outs, tok)
+
+    sc_ = lambda v: v[0] if isinstance(v, tuple) else v
+
+    def tt(o, a, b, f):
+        op("v", lambda: g.vector.tensor_tensor(o[0], a[0], b[0], f), [a, b], [o])
+
+    def ts(o, a, f, s, f2=None, s2=None):
+        if f2 is None:
+            op("v", lambda: g.vector.tensor_scalar(o[0], a[0], sc_(s), None, f), [a, s], [o])
+        else:
+            op("v", lambda: g.vector.tensor_scalar(o[0], a[0], sc_(s), sc_(s2), f, f2), [a, s, s2], [o])
+
+    def cp(o, a):
+        op("v", lambda: g.vector.tensor_copy(o[0], a[0]), [a], [o])
+
+    def act(o, a, bias=0.0, scale=1.0):
+        op("s", lambda: g.scalar.activation(o[0], a[0], F.Identity, bias=sc_(bias), scale=scale), [a, bias], [o])
+
+    def fill(o, c):
+        op("v", lambda: g.vector.memset(o[0], c), [], [o])
+
+    def mm(o, calls, ins):
+        def fn():
+            last = None
+            for c in calls:
+                last = g.tensor.matmul(*c)
+            return last
+        op("t", fn, ins, [o])
+
+    others = [k for k in range(4) if k != me]
+    off = [k for k in others if topo.chip(T.cores[k]) != topo.chip(core)]
+    on = [k for k in others if k not in off]
+    eo = topo.engines(core, T.cores[off[0]])
+    el = [e for e in topo.engines(core, T.cores[on[0]]) if e not in eo]
+    eng = {}
+    for ks, es in ((off, eo), (on, el)):
+        n = len(es) // len(ks)
+        for j, k in enumerate(ks):
+            eng[k] = es[j * n:j * n + n]
+    ARR = len(eo) + len(el)
+    nloc = [0]
+
+    def send(sem, need, src, dst):
+        waits("g", "dma", [need], [])
+        tr = []
+        for k in others:
+            rid, pid, _se = topo.addr(T.cores[k])
+            tr.append(RemoteDMATransfer(dst_ids=[DstId(rid=rid, pnc=pid)], dma_engine_mask=sum(1 << e for e in eng[k]), remote_sem=T.sem[sem], src=src(k), dst=dst))
+            nloc[0] += len(eng[k])
+        g.remote_dma_fused(tr, local_sem=T.sem["r_loc"])
+
+    def rwait(buf, lo, hi, sem):
+        allsem[sem] = ARR
+        hist.setdefault(buf, []).append((lo, hi, True, "remote", (sem, ARR)))
+
+    SO = [(s, o) for s in range(2) for o in range(4)]
+    rows = lambda s, o: slice(64 * s + 16 * o, 64 * s + 16 * o + 16)
+    mine = lambda s: slice(32 * me + 16 * s, 32 * me + 16 * s + 16)
+    CG = [T.cg0, T.cg1, T.cg2]
+    own = slice(192 * me, 192 * me + 192)
+
+    def fetch(t, q):
+        dma(q, [(T.cr[:, :, t, :, m, :], T.cand[:, 768 * t + 256 * m:768 * t + 256 * m + 256]) for m in range(3)], [], [("cr", t, t + 1)])
+
+    def stage(t, qs):
+        dma(qs, [(T.sc[4 * t:4 * t + 4, rows(s, o), :], T.cr[:, 16 * s:16 * s + 16, t, o]) for s, o in SO], [("cr", t, t + 1)], [("sc", t, t + 1)])
+
+    dma("y", [(T.sr[:], T.ray[:])], [], [("sr", 0, 4)])
+    fetch(0, "s")
+    stage(0, "sy")
+    dma("y", [(T.sp[:], T.px[:])], [], [("sp", 0, 4)])
+    dma("s", [(T.cg0[:, own], T.sc[me])], [("sc", 0, 1)], [("cg0", 0, 768)])
+    dma("s", [(T.tho[:], T.th[:]), (T.thl[:, me:me + 1], T.th[:])], [], [("tho", 0, 1), ("thl", 0, 4)])
+    for n, w, pat, base, cm in (("it1", 143, [[1, 143]], -15, -1), ("it0", 143, [[1, 143]], 0, 0), ("pc", 1, [[0, 1]], 0, 1), ("vci", 384, [[0, 12], [16, 32]], -255, 0)):
+        op("g", lambda: g.iota(T[n][:, 0:w], pat, base, cm), [], [R(n)])
+    send("r_ray", ("sr", 0, 4), lambda k: T.sr[k], T.lr[me])
+    send("r_c0", ("sc", 0, 1), lambda k: T.sc[k], T.cg0[:, own])
+    send("r_px", ("sp", 0, 4), lambda k: T.sp[k], T.lp[me])
+    send("r_th", ("tho", 0, 1), lambda k: T.tho[:], T.thl[:, me:me + 1])
+    rwait("lr", 0, 4, "r_ray")
+    rwait("cg0", 0, 768, "r_c0")
+    rwait("lp", 0, 4, "r_px")
+    rwait("thl", 0, 4, "r_th")
+
+    fill(R("wt"), 0.0)
+    ts(R("lane"), R("pc"), A.bitwise_and, 15)
+    ts(R("grp"), R("pc"), A.arith_shift_right, 4)
+    cp(R("lanef"), R("lane"))
+    ts(R("oi"), R("grp"), A.bitwise_and, 3)
+    cp(R("grpf"), R("grp"))
+    ts(R("k0"), R("lane"), A.is_equal, 0)
+    cp(R("of"), R("oi"))
+    ts(R("nk0"), R("k0"), A.mult, -1.0)
+    ts(R("g16"), R("grpf"), A.mult, 16.0, A.add, 15.0)
+    for h in range(2):
+        ts(R("nb", h, h + 1), R("of"), A.mult, -1024.0, A.add, -(512.0 * h + 255.0))
+        ts(R("pb", h, h + 1), R("of"), A.mult, 1024.0, A.add, 512.0 * h + 255.0)
+    ts(R("xi4"), R("it0", 4, 8), A.subtract, R("of"))
+    ts(R("cole"), R("of"), A.mult, -1024.0, A.add, 4096.0)
+    ts(R("xj4"), R("xi4"), A.bitwise_and, 3)
+    ts(R("colx"), R("xj4"), A.mult, 2048.0)
+    ts(R("mcb", 0, 143), R("it1", 0, 143), A.is_equal, 0, A.mult, R("nk0"))
+    ts(R("mid"), R("it1", 15, 143), A.is_equal, 0)
+    ts(R("vct"), R("vci"), A.add, R("lanef"))
+
+    dma("y", [(T.rayi[rows(s, a), :], T.ray[mine(s), :] if a == me else T.lr[a, 64 * s:64 * s + 64, :]) for s, a in SO], [("lr", 0, 4)], [("rayi", 0, 768)])
+    L = ["la", "lb"]
+
+    def place_lists(n):
+        cp(R("ln"), R(n, 0, 256))
+        ts(R("zi"), R(n, 0, 256), A.add, R("cole"))
+        ts(R("zi"), R("zi"), A.bitwise_and, 4095)
+        ts(R("zf"), R("zi"), A.add, -4096.0)
+
+    def consts():
+        ts(R("mb2", 0, 143), R("it0", 0, 143), A.subtract, R("g16"), A.is_equal, 0.0)
+        ts(R("ish"), R("it1", 15, 143), A.arith_shift_right, 4)
+        ts(R("im16"), R("it0", 0, 128), A.arith_shift_right, 4)
+        ts(R("lmk"), R("it0", 0, 16), A.is_equal, R("lanef"))
+        ts(R("mgt"), R("it1", 15, 143), A.is_gt, 0)
+        ts(R("mbc"), R("ish"), A.is_equal, 0, A.mult, R("k0"))
+        ts(R("mbo"), R("im16"), A.is_equal, R("grpf"))
+        fill(R("mt"), 0.0)
+        tt(R("mtri"), R("mbo"), R("mgt"), A.mult)
+        for i in range(16):
+            ts(R("mex", 128 * i, 128 * i + 128), R("mbo"), A.mult, R("lmk", i, i + 1))
+        fill(R("et", 4096, 4104), 0.0)
+        fill(R("zz"), 0.0)
+        fill(R("cu", 0, 16), 0.0)
+        fill(R("cc"), 0.0)
+        cp(R("la", 128, 768), R("rayi", 128, 768))
+        place_lists("la")
+
+    def table_w(n):
+        dma("y", [(T.wt[64 * s + 16 * a:64 * s + 16 * a + 1, :], T[n][64 * s:64 * s + 64, 0:128]) for s, a in SO], [(n, 0, 128)], [("wt", 0, 8192)])
+
+    def spread(n, lo, w, width):
+        items = []
+        b = T[n]
+        for d in (1, 2, 3):
+            c = d * width + lo
+            for p in (0, 64):
+                k = p + 16 * (4 - d)
+                items.append((b[p:k, c:c + w], b[p + 16 * d:p + 64, lo:lo + w]))
+                items.append((b[k:p + 64, c:c + w], b[p:p + 16 * d, lo:lo + w]))
+        dma("y", items, [(n, lo, lo + w)], [(n, d * width + lo, d * width + lo + w) for d in (1, 2, 3)])
+
+    def prep(t, b):
+        c, lw, p = R("cg%d" % t), "lw%d" % t, R(b, 0, 768)
+        ts(R("ca"), c, A.bitwise_and, 15)
+        ts(p, R("ca"), A.mult, 2047.0)
+        tt(p, c, p, A.add)
+        for a in range(4):
+            ts(R(lw, 192 * a, 192 * a + 192), R(b, 192 * a, 192 * a + 192), A.mult, 0.0625, A.add, 2048.0 * a)
+
+    def prepx(t):
+        for h in range(2):
+            for k in range(12):
+                c = 384 * h + 32 * k
+                ts(R("xb%d" % t, c, c + 32), R("cg%d" % t, 64 * k + 32 * h, 64 * k + 32 * h + 32), A.add, R("colx", k // 3, k // 3 + 1))
+
+    cp(R("la", 0, 128), R("rayi", 0, 128))
+    table_w("la")
+    prep(0, "pA")
+    dma("y", [(T.xi[rows(s, a), :], T.px[mine(s), :] if a == me else T.lp[a, 64 * s:64 * s + 64, :]) for s, a in SO], [("lp", 0, 4)], [("xi", 0, 2048)])
+
+    def look_w(t, h, ks, q):
+        for k in ks:
+            o = R("wr", 6144 * h + 512 * k, 6144 * h + 512 * k + 512)
+            src = ind(R("wt"), R("lw%d" % t, 64 * k + 32 * h, 64 * k + 32 * h + 32))
+            if q == "s":
+                act(o, src, bias=R("nb", h, h + 1))
+            else:
+                ts(o, src, A.subtract, R("pb", h, h + 1))
+
+    def list_form(h, j):
+        o, w0 = R("pB", 512 * h + 96 * j, 512 * h + 96 * j + 96), 6144 * h + 1536 * j
+        mm(o, [(o[0], T.mid[:], T.vct[:, 0:96], True, False)] + [(o[0], T.mcb[:, 15 - i:143 - i], T.wr[:, w0 + i:w0 + 1536:16], False, i == 15) for i in range(16)],
+           [R("mid"), R("vct"), R("mcb"), R("wr", w0, w0 + 1536)])
+
+    def lists(t, h):
+        p, E = R("pB", 512 * h, 512 * h + 384), R("le")
+        yield ts(p, p, A.max, 0.0, A.mult, 8192.0)
+        yield tt(E, R("xb%d" % t, 384 * h, 384 * h + 384), p, A.subtract)
+        yield tt(R("l1"), R("le", 0, 192), R("le", 192, 384), A.max)
+        yield tt(R("l2"), R("l1", 0, 96), R("l1", 96, 192), A.max)
+        yield tt(R("l3"), R("l2", 0, 32), R("l2", 32, 64), A.max)
+        tt(R("lm", 0, 32), R("l3"), R("l2", 64, 96), A.max)
+        yield tt(R("lm", 32, 64), R("l3"), R("l2", 64, 96), A.max)
+        yield cp(R("lm", 64, 128), R("lm", 0, 64))
+        cp(R("lm", 128, 256), R("lm", 0, 128))
+        yield cp(R("lm", 256, 384), R("lm", 0, 128))
+        yield tt(p, p, R("lm"), A.min)
+        yield tt(R("le2"), E, p, A.max)
+        yield cp(R("lx", 384 * h, 384 * h + 384), R("le2"))
+
+    def acc(h):
+        return R("pA", 1024 * h, 1024 * h + 512), R("pA", 1024 * h + 512, 1024 * h + 1024)
+
+    def gather_x(h, k):
+        j = 512 * ((12 * h + k) % 8)
+        G = R("xg", j, j + 512)
+        act(G, ind(R("xw"), R("lx", 384 * h + 32 * k, 384 * h + 32 * k + 32)))
+        if k == 0:
+            act(acc(h)[1], G)
+
+    def minmax(h, k):
+        j = 512 * ((12 * h + k) % 8)
+        G = R("xg", j, j + 512)
+        lo, hi = acc(h)
+        if k:
+            tt(R("et", 512 * h, 512 * h + 512) if k == 11 else lo, G, hi if k == 1 else lo, A.min)
+            tt(hi, G, hi, A.max)
+
+    def flags(h):
+        c = 512 * h
+        lt, fl = R("lt", c, c + 512), R("fl", c, c + 512)
+        act(lt, R("et", c, c + 512), bias=R("thf"))
+        tt(fl, acc(h)[1], lt, A.is_gt)
+        mm(R("pC", 0, 64), [(T.pC[:, 0:64], T.mb2[:, 15 - i:143 - i], T.fl[:, 64 * i:64 * i + 64], i == 0, i == 15) for i in range(8 * h, 8 * h + 8)], [fl, R("mb2")])
+
+    f1, f2 = R("f1"), R("pD", 0, 128)
+
+    def place(k, old, new):
+        c = 128 * k
+        tt(R("fu"), R("dd", c, c + 128), f1, A.mult)
+        tt(R("pD", 128, 256), R("dd", c + 128, c + 256), f2, A.mult)
+        tt(R("fu"), R("fu"), R(old, c, c + 128), A.add)
+        tt(R(new, c, c + 128), R("fu"), R("pD", 128, 256), A.add)
+
+    def cursors():
+        tt(R("cc"), R("cc"), f1, A.add)
+        tt(R("cc"), R("cc"), f2, A.add)
+
+    def flag(st, c):
+        b, l0 = 2048 * st + 1024 * c, 128 * st + 64 * c
+        act(R("wr", b, b + 1024), ind(R("mt"), R("ln", l0, l0 + 64)), bias=1.0, scale=0.25)
+        o = R(("pC", "pD")[st], 64 * c, 64 * c + 64)
+        mm(o, [(o[0], T.mcb[:, 15 - i:143 - i], T.wr[:, b + i:b + 1024:16], i == 0, i == 15) for i in range(16)], [R("wr", b, b + 1024), R("mcb")])
+
+    def colour(st, x0, x1):
+        b = 2048 * st
+        act(R("eg", b + x0, b + x1), ind(R("et"), R("oe", (b + x0) // 16, (b + x1) // 16)), bias=-0.375, scale=-0.25)
+
+    def colour_list(st, f):
+        c = 128 * st
+        tt(R("ft", c, c + 128), R("zf", c, c + 128), f, A.mult)
+        ts(R("oe", c, c + 128), R("ft", c, c + 128), A.add, 4096.0)
+
+    def step(st, x0, x1):
+        x, m, y = R("xw", x0, x1), R("pA", x0, x1), R("xi", x0, x1)
+        if st == 1:
+            for b in range(x0 // 512, x1 // 512):
+                mm(R("pA", 512 * b, 512 * b + 512), [(T.pA[:, 512 * b + i:512 * b + 512:16], T.mex[:, 128 * i:128 * i + 128], T.m2[:, 32 * b:32 * b + 32], True, True)
+                                                     for i in range(16)], [R("mex"), R("m2")])
+            tt(m, x, m, A.mult)
+        tt(y, R("eg", 2048 * st + x0, 2048 * st + x1), m, A.add)
+        ts(x, y, A.max, 0.0, A.min, float(TOP))
+
+    KEEP = (4, 2, 0)
+    for t in range(3):
+        last = t == 2
+        old, new = L[t % 2], L[1 - t % 2]
+        late = [j for j in range(4) if 3 * j + 3 > 12 - VSHARE]
+        for h in range(2):
+            for j in range(4):
+                look_w(t, h, [k for k in range(3 * j, 3 * j + 3) if h == 0 or k < 12 - VSHARE], "s")
+                if h == 0 or j not in late:
+                    list_form(h, j)
+        if t == 0:
+            prepx(0)
+            consts()
+            cp(R("xw", 0, 1024), R("xi", 0, 1024))
+            spread("xw", 0, 1024, 2048)
+            cp(R("xw", 1024, 2048), R("xi", 1024, 2048))
+            spread("xw", 1024, 1024, 2048)
+            dma("y", [(T.thi[rows(s, o), :], T.thl[mine(s), o:o + 1]) for s, o in SO], [("thl", 0, 4)], [("thi", 0, 1)])
+            for u in (1, 2):
+                fetch(u, "y")
+                stage(u, "y")
+                dma("y", [(CG[u][:, own], T.sc[4 * u + me])], [("sc", u, u + 1)], [("cg%d" % u, 0, 768)])
+                send("r_c%d" % u, ("sc", u, u + 1), lambda k: T.sc[4 * u + k], CG[u][:, own])
+                rwait("cg%d" % u, 0, 768, "r_c%d" % u)
+        else:
+            for k in range(1, KEEP[t - 1]):
+                place(k, new, old)
+            cursors()
+            place_lists(old)
+        for _ in lists(t, 0):
+            pass
+        look_w(t, 1, range(12 - VSHARE, 12), "v")
+        for j in late:
+            list_form(1, j)
+        gen = lists(t, 1)
+        for k in range(12):
+            gather_x(0, k)
+            minmax(0, k)
+            if k > 2:
+                next(gen, None)
+                next(gen, None)
+        for _ in gen:
+            pass
+        if t == 0:
+            cp(R("thf"), R("thi"))
+        if not last:
+            w = 128 * (KEEP[t] + 1)
+            tt(R("dd", 0, w), R(old, 128, 128 + w), R(old, 0, w), A.subtract)
+        spread("et", 0, 512, 1024)
+        for k in range(12):
+            gather_x(1, k)
+            if k == 2:
+                flags(0)
+            minmax(1, k)
+        flags(1)
+        ts(R("odd"), R("pC", 0, 64), A.is_ge, 9.0)
+        op("v", lambda: g.vector.tensor_tensor_scan(T.cu[:, 16:80], T.odd[:], T.zz[:], 0.0, A.add, A.max), [R("odd"), R("zz")], [R("cu", 16, 80)])
+        mm(R("pD", 0, 1), [(T.pD[:, 0:1], T.mtri[:], T.cu[:, 79:80], True, True)], [R("cu", 16, 80), R("mtri")])
+        ts(R("cs", 15, 80), R("cu", 15, 80), A.add, R("pD", 0, 1), A.min, 256.0)
+        tt(R("cv"), R("cs", 16, 80), R("cs", 15, 79), A.subtract)
+        dma("ys", [(T.mt[64 * s + 16 * a:64 * s + 16 * a + 1, :], T.cv[64 * s:64 * s + 64, :]) for s, a in SO], [("cv", 0, 64)], [("mt", 0, 4096)])
+        spread("et", 512, 512, 1024)
+        if not last:
+            prep(t + 1, "pB")
+            prepx(t + 1)
+        ch = CHUNKS_END if last else CHUNKS
+        flag(0, 0)
+        flag(0, 1)
+        for b in range(0, 2048, 512):
+            o = R("pA", b, b + 512)
+            mm(o, [(o[0], T.mbc[:], T.wr[:, b:b + 512], True, True)], [R("wr", b, b + 512), R("mbc")])
+        flag(1, 0)
+        flag(1, 1)
+        ts(f1, R("pC", 0, 128), A.mult, -4.0, A.add, -4.0)
+        colour_list(0, f1)
+        for x0, x1 in ch:
+            tt(R("pA", x0, x1), R("xw", x0, x1), R("pA", x0, x1), A.mult)
+        ts(f2, f2, A.mult, -4.0, A.add, -4.0)
+        tt(f2, f1, f2, A.mult)
+        colour_list(1, f2)
+        ts(R("m2"), f2, A.mult, 0.25, A.add, 1.0)
+        for c in ch:
+            colour(0, *c)
+            colour(1, *c)
+        if not last:
+            place(0, old, new)
+            table_w(new)
+        else:
+            cursors()
+            ts(R("cf"), R("cc"), A.min, 5.0)
+            dma("y", [(T.sy[a, 64 * s:64 * s + 64, :], T.cf[rows(s, a), :]) for s, a in SO if a != me], [("cf", 0, 128)], [("sy", 0, 4)])
+            dma("y", [(T.yc[mine(s), :], T.cf[rows(s, me), :]) for s in range(2)], [("cf", 0, 128)], [])
+            send("r_yc", ("sy", 0, 4), lambda k: T.sy[k], T.ly[me])
+            rwait("ly", 0, 4, "r_yc")
+        for x0, x1 in ch:
+            step(0, x0, x1)
+            step(1, x0, x1)
+            if not last:
+                spread("xw", x0, x1 - x0, 2048)
+            else:
+                c, x = x0 // 512, [("xw", x0, x1)]
+                dma("ys", [(T.so[4 * c + a, 64 * s:64 * s + 64, :], T.xw[rows(s, a), x0:x1]) for s, a in SO if a != me], x, [("so", 4 * c, 4 * c + 4)])
+                dma("y", [(T.yx[mine(s), x0:x1], T.xw[rows(s, me), x0:x1]) for s in range(2)], x, [])
+                send("r_x%d" % c, ("so", 4 * c, 4 * c + 4), lambda k: T.so[4 * c + k], T.lo[4 * c + me])
+                rwait("lo", 4 * c, 4 * c + 4, "r_x%d" % c)
+
+    dma("y", [(T.yc[32 * k:32 * k + 32, :], T.ly[k]) for k in others], [("ly", 0, 4)], [])
+    for c in range(4):
+        dma("ys", [(T.yx[32 * k:32 * k + 32, 512 * c:512 * c + 512], T.lo[4 * c + k]) for k in others], [("lo", 4 * c, 4 * c + 4)], [])
+    g.wait_ge(T.sem["r_loc"], nloc[0])
+    for s in sorted(allsem):
+        wait("y", (s, allsem[s]))

@@ -1,7 +1,8 @@
 from concourse.bass import DstId, RemoteDMATransfer
-from concourse.mybir import AluOpType as A, ActivationFunctionType as F
+from concourse.mybir import AluOpType as A, ActivationFunctionType as F, AxisListType as X
 
 TOP = 2 ** 20 - 1
+BIG = 16384.0
 SCRATCH = {}
 
 
@@ -10,28 +11,46 @@ def _buf(where, dtype, **shapes):
         SCRATCH[n] = (where, s if isinstance(s, list) else [128, s], dtype)
 
 
-_buf("dram", "int32", sp=[4, 128, 512], lp=[4, 128, 512], sr=[4, 128, 192], lr=[4, 128, 192], cr=[4, 32, 3, 4, 3, 64], sc=[12, 128, 192])
-_buf("dram", "float32", so=[16, 128, 128], lo=[16, 128, 128], sy=[4, 128, 32], ly=[4, 128, 32])
-_buf("sbuf", "int32", cg0=768, cg1=768, cg2=768, ca=768, xi=2048, rayi=768, tho=1, thl=4, thi=1,
-     zi=256, it0=144, it1=144, vci=384, pc=1, lane=1, grp=1, oi=1, xi4=4, xj4=4, ish=128, im16=128)
-_buf("sbuf", "uint16", lw0=768, lw1=768, lw2=768, lx=768, ln=256, oe=256)
-_buf("sbuf", "bfloat16", wr=12288, fl=1024, m2=128, mcb=144, mid=128, mb2=144, mbc=128, mex=2048, vct=384)
-_buf("sbuf", "float32", xb0=768, xb1=768, xb2=768, thf=1, xw=8192, wt=8192, mt=4096, et=4104, xg=4096, le=384, l1=192, l2=96,
-     l3=32, lm=384, le2=384, lt=1024, odd=64, zz=64, cu=80, cs=80, cv=64, eg=4096, la=768, lb=768, dd=640, zf=256, f1=128, ft=256, fu=128,
-     cc=128, cf=128, lanef=1, grpf=1, of=1, k0=1, nk0=1, g16=1, nb=2, pb=2, colx=4, cole=1, lmk=16, mbo=128, mgt=128, mtri=128)
-_buf("psum", "float32", pA=2048, pB=1024, pC=512, pD=512)
-PSUM = ("pA", "pB", "pC", "pD")
+S0, R1, ET, R2 = 0, 8192, 10240, 14336
+_buf("dram", "int32", sr=[4, 128, 192], lr=[4, 128, 192])
+_buf("dram", "float32", lp=[8, 128, 256], ly=[4, 128, 512], lc=[4, 128, 32])
+_buf("sbuf", "int32", cq=[128, 36, 2, 32], xi=2048, tho=1, zi=256, it0=144, it1=144, vci=96, pc=1, lane=1, grp=1, oi=1, ji=128, ip=128, iq=128)
+_buf("sbuf", "uint16", lw0=[128, 8, 96], lws=[128, 4, 12, 32], lwt=1536, lwr=[128, 4, 384], lx=768, ln=256, oe=256)
+_buf("sbuf", "bfloat16", wr=6144, mt=4096, fl=1024, mcb=144, mid=128, mb2=144, vct=96, jh=128, cv=64, msel=512, mp=256)
+_buf("sbuf", "float32", B=16384, wt=8192, xg=6144, eg=4096, es=[128, 8, 100], el=800, er=[128, 8, 100],
+     xbs=[128, 4, 12, 32], xbr=[128, 4, 384], le=384, l1=192, l2=96, l3=32, lm=96, le2=384, thf=1, odd=64, zz=64, cu=80, cs=80,
+     la=768, lb=512, lz=[128, 3, 4, 32], lq=[128, 3, 4, 32], dd=640, ce=128, zf=128, sj=128, f1=128, ft=128, fu=128, cc=128, cf=128, wp=128,
+     lanef=1, grpf=1, of=1, k0=1, nk0=1, g16=1, nb=2, pb=2, cole=1, col1=1, mtri=128, mper=128)
+_buf("psum", "float32", pA=2048, pD=1024, pC=512, pE=512)
+PSUM = ("pA", "pD", "pC", "pE")
 ENG = {"v": "q_v", "s": "q_s", "t": "q_t", "g": "q_g"}
-DSEM = ["d%d" % j for j in range(64)]
-SEMAPHORES = list(ENG.values()) + DSEM + ["r_ray", "r_c0", "r_px", "r_th", "r_c1", "r_c2", "r_yc", "r_x0", "r_x1", "r_x2", "r_x3", "r_loc"]
-VSHARE = 3
-CHUNKS = ((0, 1024), (1024, 2048))
-CHUNKS_END = ((0, 512), (512, 1024), (1024, 1536), (1536, 2048))
+DSEM = ["d%d" % j for j in range(100)]
+SEMAPHORES = list(ENG.values()) + DSEM + ["r_p0", "r_p1", "r_e0", "r_e1", "r_ray", "r_lw", "r_xb", "r_yc", "r_x0", "r_x1", "r_x2", "r_x3",
+                                          "r_f0", "r_f1", "r_f2", "l_px", "l_list", "l_end"]
+FIVE = 2
+FOLD = 2
+
+
+def helper(core, T, topo):
+    free = [c for c in topo.cores_of(core) if c not in T.cores and topo.die(c) == topo.die(core)]
+    return free[0]
+
+
+def mask(es):
+    return sum(1 << e for e in es)
 
 
 def rank_program(g, core, T, topo):
     me = T.rank_of(core)
     if me is None:
+        for c in T.cores:
+            if FOLD and helper(c, T, topo) == core:
+                rid, pid, _se = topo.addr(c)
+                es = topo.engines(core, c)
+                for t in range(3):
+                    g.wait_ge(T.sem["r_f%d" % t], len(es))
+                    g.remote_dma(T.B[:, R2 + 1024:R2 + 2048], T.xg[:, 1024 * t:1024 * t + 1024], T.sem["r_f%d" % t], T.sem["l_end"], pid, rid, mask(es))
+                g.wait_ge(T.sem["l_end"], 3 * len(es))
         return
     Q = {"v": g.vector, "s": g.scalar, "t": g.tensor, "y": g.sync, "g": g}
     known = {q: {} for q in Q}
@@ -65,15 +84,18 @@ def rank_program(g, core, T, topo):
         for s in sorted(toks):
             wait(q, (s, toks[s]))
 
-    def note(q, reads, writes, tok):
+    def note(q, reads, writes, tok, apart=False):
         for buf, lo, hi in writes:
-            hist[buf] = [e for e in hist.get(buf, ()) if not (lo <= e[0] and e[1] <= hi)] + [(lo, hi, True, q, tok)]
+            hist[buf] = [e for e in hist.get(buf, ()) if apart or not (lo <= e[0] and e[1] <= hi)] + [(lo, hi, True, q, tok)]
         for buf, lo, hi in reads:
             hist[buf] = [e for e in hist.get(buf, ()) if not (lo <= e[0] and e[1] <= hi and not e[2] and e[3] == q and q in ENG)] + [(lo, hi, False, q, tok)]
 
     def R(n, a=0, b=None):
         b = SCRATCH[n][1][-1] if b is None else b
         return (T[n][:, a:b], [(n, a, b)])
+
+    def V(ap, n, a=0, b=1 << 20):
+        return (ap, [(n, a, b)])
 
     def ind(win, off):
         return (win[0].indirect(off[0]), win[1] + off[1])
@@ -90,12 +112,12 @@ def rank_program(g, core, T, topo):
         snap[tok] = dict(known[q])
         note(q, rd, wr, tok)
 
-    def dma(qs, items, ins, outs):
+    def dma(qs, items, ins, outs, apart=False):
         sem = DSEM[nd[0]]
         nd[0] += 1
         kn = {}
         for q in qs:
-            waits(q, "dma", ins, outs)
+            waits(q, "dma", ins, [] if apart else outs)
             for s, v in known[q].items():
                 kn[s] = max(kn.get(s, 0), v)
         for j, (o, i) in enumerate(items):
@@ -103,7 +125,7 @@ def rank_program(g, core, T, topo):
         tok = (sem, 16 * len(items))
         allsem[sem] = tok[1]
         snap[tok] = kn
-        note("dma", ins, outs, tok)
+        note("dma", ins, outs, tok, apart)
 
     sc_ = lambda v: v[0] if isinstance(v, tuple) else v
 
@@ -133,8 +155,13 @@ def rank_program(g, core, T, topo):
             return last
         op("t", fn, ins, [o])
 
+    def run(gen, n=99):
+        for _ in range(n):
+            next(gen, None)
+
     others = [k for k in range(4) if k != me]
-    off = [k for k in others if topo.chip(T.cores[k]) != topo.chip(core)]
+    far = lambda a, b: topo.chip(T.cores[a]) != topo.chip(T.cores[b])
+    off = [k for k in others if far(k, me)]
     on = [k for k in others if k not in off]
     eo = topo.engines(core, T.cores[off[0]])
     el = [e for e in topo.engines(core, T.cores[on[0]]) if e not in eo]
@@ -144,334 +171,449 @@ def rank_program(g, core, T, topo):
         for j, k in enumerate(ks):
             eng[k] = es[j * n:j * n + n]
     ARR = len(eo) + len(el)
-    nloc = [0]
+    SENT = {"l_px": 2 * ARR, "l_list": 5 * ARR}
+    nend = [0]
 
-    def send(sem, need, src, dst):
+    def transfer(k, es, sem, src, dst):
+        rid, pid, _se = topo.addr(T.cores[k])
+        return RemoteDMATransfer(dst_ids=[DstId(rid=rid, pnc=pid)], dma_engine_mask=mask(es), remote_sem=T.sem[sem], src=src, dst=dst)
+
+    def send(sem, need, src, dst, land, loc):
         waits("g", "dma", [need], [])
-        tr = []
-        for k in others:
-            rid, pid, _se = topo.addr(T.cores[k])
-            tr.append(RemoteDMATransfer(dst_ids=[DstId(rid=rid, pnc=pid)], dma_engine_mask=sum(1 << e for e in eng[k]), remote_sem=T.sem[sem], src=src(k), dst=dst))
-            nloc[0] += len(eng[k])
-        g.remote_dma_fused(tr, local_sem=T.sem["r_loc"])
+        g.remote_dma_fused([transfer(k, eng[k], sem, src(k), dst) for k in others], local_sem=T.sem[loc])
+        if loc in SENT:
+            hist[need[0]].append((need[1], need[2], False, "remote", (loc, SENT[loc])))
+        else:
+            nend[0] += ARR
+        arrive(land, sem, ARR)
 
-    def rwait(buf, lo, hi, sem):
-        allsem[sem] = ARR
-        hist.setdefault(buf, []).append((lo, hi, True, "remote", (sem, ARR)))
+    def arrive(land, sem, n):
+        allsem[sem] = n
+        hist.setdefault(land[0], []).append((land[1], land[2], True, "remote", (sem, n)))
 
-    SO = [(s, o) for s in range(2) for o in range(4)]
-    rows = lambda s, o: slice(64 * s + 16 * o, 64 * s + 16 * o + 16)
-    mine = lambda s: slice(32 * me + 16 * s, 32 * me + 16 * s + 16)
-    CG = [T.cg0, T.cg1, T.cg2]
-    own = slice(192 * me, 192 * me + 192)
+    rows = lambda o: slice(32 * o, 32 * o + 32)
+    order = off + on + [me]
+    four = range(4)
 
-    def fetch(t, q):
-        dma(q, [(T.cr[:, :, t, :, m, :], T.cand[:, 768 * t + 256 * m:768 * t + 256 * m + 256]) for m in range(3)], [], [("cr", t, t + 1)])
-
-    def stage(t, qs):
-        dma(qs, [(T.sc[4 * t:4 * t + 4, rows(s, o), :], T.cr[:, 16 * s:16 * s + 16, t, o]) for s, o in SO], [("cr", t, t + 1)], [("sc", t, t + 1)])
-
-    dma("y", [(T.sr[:], T.ray[:])], [], [("sr", 0, 4)])
-    fetch(0, "s")
-    stage(0, "sy")
-    dma("y", [(T.sp[:], T.px[:])], [], [("sp", 0, 4)])
-    dma("s", [(T.cg0[:, own], T.sc[me])], [("sc", 0, 1)], [("cg0", 0, 768)])
-    dma("s", [(T.tho[:], T.th[:]), (T.thl[:, me:me + 1], T.th[:])], [], [("tho", 0, 1), ("thl", 0, 4)])
-    for n, w, pat, base, cm in (("it1", 143, [[1, 143]], -15, -1), ("it0", 143, [[1, 143]], 0, 0), ("pc", 1, [[0, 1]], 0, 1), ("vci", 384, [[0, 12], [16, 32]], -255, 0)):
-        op("g", lambda: g.iota(T[n][:, 0:w], pat, base, cm), [], [R(n)])
-    send("r_ray", ("sr", 0, 4), lambda k: T.sr[k], T.lr[me])
-    send("r_c0", ("sc", 0, 1), lambda k: T.sc[k], T.cg0[:, own])
-    send("r_px", ("sp", 0, 4), lambda k: T.sp[k], T.lp[me])
-    send("r_th", ("tho", 0, 1), lambda k: T.tho[:], T.thl[:, me:me + 1])
-    rwait("lr", 0, 4, "r_ray")
-    rwait("cg0", 0, 768, "r_c0")
-    rwait("lp", 0, 4, "r_px")
-    rwait("thl", 0, 4, "r_th")
-
-    fill(R("wt"), 0.0)
+    dma("s", [(T.zi[:, 0:128], T.ray[:, 0:128])], [], [("zi", 0, 128)])
+    dma("s", [(T.cq[:, 0:12], T.cand[:, 0:768])], [], [("cq", 0, 768)])
+    for hf in range(2):
+        dma("ys"[hf], [(T.xi[:, 1024 * hf + 256 * k:1024 * hf + 256 * k + 256], T.px[rows(k), 1024 * hf:1024 * hf + 1024]) for k in order],
+            [], [("xi", 1024 * hf, 1024 * hf + 1024)])
+    dma("s", [(T.tho[:], T.th[:])], [], [("tho", 0, 1)])
+    for n, a, b, pat, base, cm in [("pc", 0, 1, [[0, 1]], 0, 1), ("it1", 0, 143, [[1, 143]], -15, -1), ("vci", 0, 96, [[0, 3], [16, 32]], -255, 0),
+                                   ("it0", 0, 143, [[1, 143]], 0, 0), ("ji", 0, 128, [[16, 128]], 0, 0), ("ip", 0, 128, [[16, 2], [32, 4], [1, 16]], 0, -1)] + [
+                                   ("iq", 32 * o, 32 * o + 32, [[16, 2], [32, 4], [4, 4]], 0, -1) for o in four]:
+        op("g", lambda: g.iota(T[n][:, a:b], pat, base, cm), [], [R(n, a, b)])
+    fill(R("wt", 0, 2048), 0.0)
     ts(R("lane"), R("pc"), A.bitwise_and, 15)
-    ts(R("grp"), R("pc"), A.arith_shift_right, 4)
+    fill(V(T.es[:], "es"), 0.0)
     cp(R("lanef"), R("lane"))
-    ts(R("oi"), R("grp"), A.bitwise_and, 3)
-    cp(R("grpf"), R("grp"))
     ts(R("k0"), R("lane"), A.is_equal, 0)
-    cp(R("of"), R("oi"))
-    ts(R("nk0"), R("k0"), A.mult, -1.0)
-    ts(R("g16"), R("grpf"), A.mult, 16.0, A.add, 15.0)
-    for h in range(2):
-        ts(R("nb", h, h + 1), R("of"), A.mult, -1024.0, A.add, -(512.0 * h + 255.0))
-        ts(R("pb", h, h + 1), R("of"), A.mult, 1024.0, A.add, 512.0 * h + 255.0)
-    ts(R("xi4"), R("it0", 4, 8), A.subtract, R("of"))
-    ts(R("cole"), R("of"), A.mult, -1024.0, A.add, 4096.0)
-    ts(R("xj4"), R("xi4"), A.bitwise_and, 3)
-    ts(R("colx"), R("xj4"), A.mult, 2048.0)
-    ts(R("mcb", 0, 143), R("it1", 0, 143), A.is_equal, 0, A.mult, R("nk0"))
-    ts(R("mid"), R("it1", 15, 143), A.is_equal, 0)
-    ts(R("vct"), R("vci"), A.add, R("lanef"))
+    cp(R("lb", 0, 128), R("zi", 0, 128))
+    dma("y", [(T.wt[0:128:16, 0:2048], T.lb[:, 0:128])], [("lb", 0, 128)], [("wt", 0, 2048)])
+    ts(R("nk0"), R("k0"), A.mult, -BIG)
 
-    dma("y", [(T.rayi[rows(s, a), :], T.ray[mine(s), :] if a == me else T.lr[a, 64 * s:64 * s + 64, :]) for s, a in SO], [("lr", 0, 4)], [("rayi", 0, 768)])
-    L = ["la", "lb"]
+    def pixels(hf):
+        c = 2048 + 1024 * hf
+        cp(R("eg", c, c + 1024), R("xi", c - 2048, c - 1024))
+        send("r_p%d" % hf, ("eg", c, c + 1024), lambda k: T.eg[:, c + 256 * k:c + 256 * k + 256], T.lp[4 * hf + me], ("lp", 4 * hf, 4 * hf + 4), "l_px")
 
-    def place_lists(n):
-        cp(R("ln"), R(n, 0, 256))
-        ts(R("zi"), R(n, 0, 256), A.add, R("cole"))
-        ts(R("zi"), R("zi"), A.bitwise_and, 4095)
-        ts(R("zf"), R("zi"), A.add, -4096.0)
+    def table_x(q, hf, who):
+        c = 1024 * hf
+        src = lambda a: T.eg[:, 2048 + c + 256 * a:2048 + c + 256 * a + 256] if a == me else T.lp[4 * hf + a]
+        col = lambda a, o: 2048 + 2048 * ((a - o - 1) % 4) + c
+        dma(q, [(T.B[rows(o), col(a, o):col(a, o) + 1024], src(a)) for a in who for o in four],
+            [("eg", 2048 + c, 3072 + c) if who == [me] else ("lp", 4 * hf, 4 * hf + 4)], [("B", 2048 * d + c, 2048 * d + c + 1024) for d in (1, 2, 3, 4)], apart=True)
+
+    def places(c, n, outs, add):
+        p = R("pA", 1024, 1024 + n)
+        ts(R("xi", 0, n), c, A.bitwise_and, 15)
+        ts(p, R("xi", 0, n), A.mult, 2047.0)
+        tt(p, c, p, A.add)
+        for m in range(3):
+            ts(outs(m), R("pA", 1024 + m * n // 3, 1024 + (m + 1) * n // 3), A.mult, 0.0625, A.add, add)
+
+    def prep0(h):
+        places(V(T.cq[:, 0:12, h, :], "cq", 0, 768), 384, lambda m: V(T.lw0[:, 4 * h:4 * h + 4, 32 * m:32 * m + 32], "lw0", h, h + 1), 0.0)
+
+    def prep(t):
+        places(V(T.cq[:, 12 * t:12 * t + 12], "cq", 768 * t, 768 * t + 768), 768, lambda m: V(T.lws[:, :, 6 * t - 6 + m:6 * t:3, :], "lws"), 2048.0 * me)
+        for o in four:
+            fill(R("pC", 64 * o, 64 * o + 64), 2048.0 * ((me - o - 2 + t) % 4))
+        for m in range(3):
+            tt(V(T.xbs[:, :, 6 * t - 6 + m:6 * t:3, :], "xbs"), V(T.cq[:, 12 * t + 4 * m:12 * t + 4 * m + 4], "cq", 768 * t, 768 * t + 768), R("pC", 0, 256), A.add)
+
+    nw = [0]
+
+    def look_w(qs, win, lst, nbias, pbias, out):
+        c, n = 1536 * (nw[0] % 4), 96 // len(qs)
+        nw[0] += 1
+        for j, q in enumerate(qs):
+            o, src = R("wr", c + 16 * n * j, c + 16 * n * (j + 1)), ind(win, lst(n * j, n * (j + 1)))
+            if q == "s":
+                act(o, src, bias=nbias)
+            else:
+                ts(o, src, A.subtract, pbias)
+            if j == len(qs) - 1:
+                mm(out, [(out[0], T.mid[:], T.vct[:], True, False)] + [(out[0], T.mcb[:, 15 - i:143 - i], T.wr[:, c + i:c + 1536:16], False, i == 15) for i in range(16)],
+                   [R("mid"), R("vct"), R("mcb"), R("wr", c, c + 1536)])
+            yield
+
+    def look0(qs, h, o):
+        b = 1024.0 * o + 512.0 * h + 255.0
+        run(look_w(qs, R("wt", 0, 2048), lambda u, v: V(T.lw0[:, 4 * h + o, u:v], "lw0", h, h + 1), -b, b, R(("pA", "pE")[h], 96 * o, 96 * o + 96)))
+
+    def seen0(h):
+        for o in four:
+            p = R(("pA", "pE")[h], 96 * o, 96 * o + 96)
+            ts(p, p, A.max, 0.0, A.subtract, 2048.0 * ((me - o - 1) % 4))
+        for o in four:
+            c = 400 * h + 100 * o
+            tt(V(T.es[:, 4 * h + o, 0:96], "es", c, c + 96), V(T.cq[:, o:12:4, h, :], "cq", 0, 768), R(("pA", "pE")[h], 96 * o, 96 * o + 96), A.subtract)
+        c = 400 * h
+        dma("y", [(T.el[rows(o), c + 100 * k:c + 100 * k + 100], T.es[rows(k), 4 * h + o, :]) for k in others for o in four], [("es", c, c + 400)], [("el", c, c + 400)])
+        send("r_e%d" % h, ("el", c, c + 400), lambda k: T.el[:, c + 100 * k:c + 100 * k + 100], T.er[:, 4 * h + me, :], ("er", c, c + 400), "l_list")
+        dma("y", [(T.er[rows(o), 4 * h + me, :], T.es[rows(me), 4 * h + o, :]) for o in four], [("es", c, c + 400)], [("er", c, c + 400)], apart=True)
 
     def consts():
+        ts(R("grp"), R("pc"), A.arith_shift_right, 4)
+        ts(R("zi", 0, 128), R("it0", 0, 128), A.arith_shift_right, 4)
+        ts(R("oi"), R("pc"), A.arith_shift_right, 5)
+        cp(R("grpf"), R("grp"))
+        cp(R("of"), R("oi"))
+        ts(R("g16"), R("grpf"), A.mult, 16.0, A.add, 15.0)
+        for h in range(2):
+            ts(R("nb", h, h + 1), R("of"), A.mult, -1024.0, A.add, -(512.0 * h + 255.0))
+            ts(R("pb", h, h + 1), R("of"), A.mult, 1024.0, A.add, 512.0 * h + 255.0)
+        ts(R("cole"), R("of"), A.mult, -1024.0, A.add, 4096.0)
+        ts(R("col1"), R("lanef"), A.mult, -1.0, A.add, 2048.0)
         ts(R("mb2", 0, 143), R("it0", 0, 143), A.subtract, R("g16"), A.is_equal, 0.0)
-        ts(R("ish"), R("it1", 15, 143), A.arith_shift_right, 4)
-        ts(R("im16"), R("it0", 0, 128), A.arith_shift_right, 4)
-        ts(R("lmk"), R("it0", 0, 16), A.is_equal, R("lanef"))
-        ts(R("mgt"), R("it1", 15, 143), A.is_gt, 0)
-        ts(R("mbc"), R("ish"), A.is_equal, 0, A.mult, R("k0"))
-        ts(R("mbo"), R("im16"), A.is_equal, R("grpf"))
-        fill(R("mt"), 0.0)
-        tt(R("mtri"), R("mbo"), R("mgt"), A.mult)
-        for i in range(16):
-            ts(R("mex", 128 * i, 128 * i + 128), R("mbo"), A.mult, R("lmk", i, i + 1))
-        fill(R("et", 4096, 4104), 0.0)
+        ts(R("fu"), R("it1", 15, 143), A.is_gt, 0)
+        ts(R("f1"), R("zi", 0, 128), A.is_equal, R("grpf"))
+        cp(R("jh"), R("ji"))
+        ts(R("sj"), R("ji"), A.add, R("lanef"), A.add, 4096.0)
+        tt(R("mtri"), R("f1"), R("fu"), A.mult)
+        ts(R("mper"), R("ip"), A.is_equal, 0)
+        for j in four:
+            ts(R("msel", 128 * j, 128 * j + 128), R("iq"), A.is_equal, -j)
         fill(R("zz"), 0.0)
         fill(R("cu", 0, 16), 0.0)
         fill(R("cc"), 0.0)
-        cp(R("la", 128, 768), R("rayi", 128, 768))
-        place_lists("la")
 
-    def table_w(n):
-        dma("y", [(T.wt[64 * s + 16 * a:64 * s + 16 * a + 1, :], T[n][64 * s:64 * s + 64, 0:128]) for s, a in SO], [(n, 0, 128)], [("wt", 0, 8192)])
+    def later():
+        for src, sn, til, tn, c, lan, ln, sem in ((T.lws, "lws", T.lwt, "lwt", 0, T.lwr, "lwr", "r_lw"), (T.xbs, "xbs", T.wt, "wt", 2048, T.xbr, "xbr", "r_xb")):
+            dma("y", [(lan[rows(o), k, :] if k == me else til[rows(o), c + 384 * k:c + 384 * k + 384], src[rows(k), o]) for k in order for o in four],
+                [(sn, 0, 1 << 20)], [(tn, c, c + 1536), (ln, 0, 1536)])
+            send(sem, (tn, c, c + 1536), lambda k: til[:, c + 384 * k:c + 384 * k + 384], lan[:, me, :], (ln, 0, 1536), "l_list")
 
-    def spread(n, lo, w, width):
-        items = []
-        b = T[n]
-        for d in (1, 2, 3):
-            c = d * width + lo
-            for p in (0, 64):
-                k = p + 16 * (4 - d)
-                items.append((b[p:k, c:c + w], b[p + 16 * d:p + 64, lo:lo + w]))
-                items.append((b[k:p + 64, c:c + w], b[p:p + 16 * d, lo:lo + w]))
-        dma("y", items, [(n, lo, lo + w)], [(n, d * width + lo, d * width + lo + w) for d in (1, 2, 3)])
+    pixels(0)
+    ts(R("mcb", 0, 143), R("it1", 0, 143), A.is_equal, 0, A.mult, R("nk0"))
+    prep0(0)
+    ts(R("mid"), R("it1", 15, 143), A.is_equal, 0)
+    ts(R("vct"), R("vci"), A.add, R("lanef"), A.mult, BIG)
+    look0("s", 0, 0)
+    look0("v", 0, 3)
+    pixels(1)
+    table_x("y", 0, [me])
+    table_x("y", 1, [me])
+    dma("y", [(T.cq[:, 12:36], T.cand[:, 768:2304])], [], [("cq", 768, 2304)])
+    cp(V(T.es[:, me, 96:97], "es", 100 * me + 96, 100 * me + 97), R("tho"))
+    look0("s", 0, 1)
+    look0("sv", 0, 2)
+    prep0(1)
+    fill(R("mt"), 0.0)
+    seen0(0)
+    table_x("y", 0, others)
+    table_x("y", 1, others)
+    for o in four:
+        look0("s", 1, o)
+    for c in (2048, 4096, 6144):
+        act(R("wt", c, c + 2048), R("wt", 0, 2048))
+    consts()
+    prep(1)
+    seen0(1)
+    dma("y", [(T.sr[:], T.ray[:])], [], [("sr", 0, 4)])
+    send("r_ray", ("sr", 0, 4), lambda k: T.sr[k], T.lr[me], ("lr", 0, 4), "l_list")
 
-    def prep(t, b):
-        c, lw, p = R("cg%d" % t), "lw%d" % t, R(b, 0, 768)
-        ts(R("ca"), c, A.bitwise_and, 15)
-        ts(p, R("ca"), A.mult, 2047.0)
-        tt(p, c, p, A.add)
-        for a in range(4):
-            ts(R(lw, 192 * a, 192 * a + 192), R(b, 192 * a, 192 * a + 192), A.mult, 0.0625, A.add, 2048.0 * a)
-
-    def prepx(t):
-        for h in range(2):
-            for k in range(12):
-                c = 384 * h + 32 * k
-                ts(R("xb%d" % t, c, c + 32), R("cg%d" % t, 64 * k + 32 * h, 64 * k + 32 * h + 32), A.add, R("colx", k // 3, k // 3 + 1))
-
-    cp(R("la", 0, 128), R("rayi", 0, 128))
-    table_w("la")
-    prep(0, "pA")
-    dma("y", [(T.xi[rows(s, a), :], T.px[mine(s), :] if a == me else T.lp[a, 64 * s:64 * s + 64, :]) for s, a in SO], [("lp", 0, 4)], [("xi", 0, 2048)])
-
-    def look_w(t, h, ks, q):
-        for k in ks:
-            o = R("wr", 6144 * h + 512 * k, 6144 * h + 512 * k + 512)
-            src = ind(R("wt"), R("lw%d" % t, 64 * k + 32 * h, 64 * k + 32 * h + 32))
-            if q == "s":
-                act(o, src, bias=R("nb", h, h + 1))
-            else:
-                ts(o, src, A.subtract, R("pb", h, h + 1))
-
-    def list_form(h, j):
-        o, w0 = R("pB", 512 * h + 96 * j, 512 * h + 96 * j + 96), 6144 * h + 1536 * j
-        mm(o, [(o[0], T.mid[:], T.vct[:, 0:96], True, False)] + [(o[0], T.mcb[:, 15 - i:143 - i], T.wr[:, w0 + i:w0 + 1536:16], False, i == 15) for i in range(16)],
-           [R("mid"), R("vct"), R("mcb"), R("wr", w0, w0 + 1536)])
+    def look(qs, t, h, a):
+        c = 192 * (t - 1) + 96 * h
+        return look_w(qs, R("wt"), lambda u, v: V(T.lwr[:, a, c + u:c + v], "lwr"), R("nb", h, h + 1), R("pb", h, h + 1), R("pD", 512 * h + 96 * a, 512 * h + 96 * a + 96))
 
     def lists(t, h):
-        p, E = R("pB", 512 * h, 512 * h + 384), R("le")
-        yield ts(p, p, A.max, 0.0, A.mult, 8192.0)
-        yield tt(E, R("xb%d" % t, 384 * h, 384 * h + 384), p, A.subtract)
-        yield tt(R("l1"), R("le", 0, 192), R("le", 192, 384), A.max)
-        yield tt(R("l2"), R("l1", 0, 96), R("l1", 96, 192), A.max)
-        yield tt(R("l3"), R("l2", 0, 32), R("l2", 32, 64), A.max)
-        tt(R("lm", 0, 32), R("l3"), R("l2", 64, 96), A.max)
-        yield tt(R("lm", 32, 64), R("l3"), R("l2", 64, 96), A.max)
-        yield cp(R("lm", 64, 128), R("lm", 0, 64))
-        cp(R("lm", 128, 256), R("lm", 0, 128))
-        yield cp(R("lm", 256, 384), R("lm", 0, 128))
-        yield tt(p, p, R("lm"), A.min)
-        yield tt(R("le2"), E, p, A.max)
-        yield cp(R("lx", 384 * h, 384 * h + 384), R("le2"))
+        p = R("pD", 512 * h, 512 * h + 384)
+        if t == 0:
+            E = lambda a, b: V(T.er[:, 4 * h + a:4 * h + b, 0:96], "er", 400 * h, 400 * h + 400)
+            ts(p, E(0, 4), A.mult, -1.0)
+        else:
+            E, c = (lambda a, b: R("le", 96 * a, 96 * b)), 192 * (t - 1) + 96 * h
+            ts(p, p, A.max, 0.0)
+            tt(E(0, 4), V(T.xbr[:, :, c:c + 96], "xbr"), p, A.subtract)
+        tt(R("l1"), E(0, 2), E(2, 4), A.max)
+        tt(R("l2"), R("l1", 0, 96), R("l1", 96, 192), A.max)
+        tt(R("l3"), R("l2", 0, 32), R("l2", 32, 64), A.max)
+        for m in range(3):
+            tt(R("lm", 32 * m, 32 * m + 32), R("l3"), R("l2", 64, 96), A.max)
+        for a in four:
+            q = R("pD", 512 * h + 96 * a, 512 * h + 96 * a + 96)
+            tt(q, q, R("lm"), A.min)
+        tt(R("le2"), E(0, 4), p, A.max)
+        cp(R("lx", 384 * h, 384 * h + 384), R("le2"))
 
     def acc(h):
         return R("pA", 1024 * h, 1024 * h + 512), R("pA", 1024 * h + 512, 1024 * h + 1024)
 
-    def gather_x(h, k):
-        j = 512 * ((12 * h + k) % 8)
-        G = R("xg", j, j + 512)
-        act(G, ind(R("xw"), R("lx", 384 * h + 32 * k, 384 * h + 32 * k + 32)))
-        if k == 0:
-            act(acc(h)[1], G)
+    first = lambda h: 0 if h else FOLD
 
-    def minmax(h, k):
-        j = 512 * ((12 * h + k) % 8)
-        G = R("xg", j, j + 512)
+    def pix(h, a, m, n):
+        return R("eg" if a < first(h) else "xg", 1536 * a + 512 * m, 1536 * a + 512 * n)
+
+    def gather_x(t, h, a):
+        c, w = 384 * h + 96 * a, (0 if t == 2 else 2048)
+        parts = ((0, 1), (1, 2), (2, 3)) if (h, a) in ((0, first(0)), (1, 3)) else ((0, 1), (1, 3)) if a == first(h) else ((0, 3),)
+        for m, n in parts:
+            act(pix(h, a, m, n), ind(R("B", w, w + 8192), R("lx", c + 32 * m, c + 32 * n)))
+            if a == first(h) and m == 0:
+                act(acc(h)[1], pix(h, a, 0, 1))
+
+    def minmax(h, a):
         lo, hi = acc(h)
-        if k:
-            tt(R("et", 512 * h, 512 * h + 512) if k == 11 else lo, G, hi if k == 1 else lo, A.min)
-            tt(hi, G, hi, A.max)
+        for m in range(3):
+            k = 3 * (a - first(h)) + m
+            if k:
+                done = (a, m) == (3, 2) and not first(h)
+                tt(R("B", ET + 512 * h, ET + 512 * h + 512) if done else lo, pix(h, a, m, m + 1), hi if k == 1 else lo, A.min)
+                tt(hi, pix(h, a, m, m + 1), hi, A.max)
+
+    def fold(t):
+        c = helper(core, T, topo)
+        rid, pid, _se = topo.addr(c)
+        es = topo.engines(core, c)
+        n = len(es) // 2
+        waits("g", "dma", [("eg", 0, 1536 * FOLD)], [("B", R2 + 1024, R2 + 2048)])
+        g.remote_dma_fused([RemoteDMATransfer(dst_ids=[DstId(rid=rid, pnc=pid)], dma_engine_mask=mask(es[j * n:j * n + n]), remote_sem=T.sem["r_f%d" % t],
+                                              srcs=[T.eg[:, 512 * k:512 * k + 512] for k in range(3 * FOLD)],
+                                              dsts=[T.xg[:, 1024 * t + 512 * j:1024 * t + 512 * j + 512]], alu_op=(3, 2)[j]) for j in range(2)], local_sem=T.sem["l_end"])
+        nend[0] += 2 * n
+        back = len(topo.engines(c, core))
+        hist["eg"].append((0, 1536 * FOLD, False, "remote", ("r_f%d" % t, back)))
+        arrive(("B", R2 + 1024, R2 + 2048), "r_f%d" % t, back)
+
+    def merge():
+        lo, hi = acc(0)
+        tt(R("B", ET, ET + 512), R("B", R2 + 1024, R2 + 1536), lo, A.min)
+        tt(hi, R("B", R2 + 1536, R2 + 2048), hi, A.max)
 
     def flags(h):
         c = 512 * h
-        lt, fl = R("lt", c, c + 512), R("fl", c, c + 512)
-        act(lt, R("et", c, c + 512), bias=R("thf"))
+        lt, fl = R("B", R2 + c, R2 + c + 512), R("fl", c, c + 512)
+        act(lt, R("B", ET + c, ET + c + 512), bias=R("thf"))
         tt(fl, acc(h)[1], lt, A.is_gt)
         mm(R("pC", 0, 64), [(T.pC[:, 0:64], T.mb2[:, 15 - i:143 - i], T.fl[:, 64 * i:64 * i + 64], i == 0, i == 15) for i in range(8 * h, 8 * h + 8)], [fl, R("mb2")])
 
-    f1, f2 = R("f1"), R("pD", 0, 128)
+    def spread(src, dst, lo, w, width):
+        items = []
+        for d in (1, 2, 3):
+            c, k = dst + d * width + lo, 32 * (4 - d)
+            items.append((T.B[0:k, c:c + w], T.B[32 * d:128, src + lo:src + lo + w]))
+            items.append((T.B[k:128, c:c + w], T.B[0:32 * d, src + lo:src + lo + w]))
+        dma("y", items, [("B", src + lo, src + lo + w)], [("B", dst + d * width + lo, dst + d * width + lo + w) for d in (1, 2, 3)])
 
-    def place(k, old, new):
+    def at(t, k, n=1):
+        if t < 2:
+            return R(("la", "lb")[t], 128 * k, 128 * (k + n))
+        return V(T.lz[:, k:k + n], "lz", k, k + n)
+
+    def place_lists(src):
+        cp(R("ln"), src)
+        ts(R("zi"), src, A.add, R("cole"))
+        ts(R("zi"), R("zi"), A.bitwise_and, 4095)
+        ts(R("ce"), R("zi", 0, 128), A.add, R("col1"))
+        tt(R("zf"), R("zi", 128, 256), R("sj"), A.subtract)
+
+    f1, f2 = R("f1"), R("pE", 0, 128)
+
+    def place(t, k):
         c = 128 * k
         tt(R("fu"), R("dd", c, c + 128), f1, A.mult)
-        tt(R("pD", 128, 256), R("dd", c + 128, c + 256), f2, A.mult)
-        tt(R("fu"), R("fu"), R(old, c, c + 128), A.add)
-        tt(R(new, c, c + 128), R("fu"), R("pD", 128, 256), A.add)
+        tt(R("pE", 128, 256), R("dd", c + 128, c + 256), f2, A.mult)
+        tt(R("fu"), R("fu"), at(t, k), A.add)
+        tt(at(t + 1, k), R("fu"), R("pE", 128, 256), A.add)
 
-    def cursors():
-        tt(R("cc"), R("cc"), f1, A.add)
-        tt(R("cc"), R("cc"), f2, A.add)
-
-    def flag(st, c):
+    def flag(q, st, c):
         b, l0 = 2048 * st + 1024 * c, 128 * st + 64 * c
-        act(R("wr", b, b + 1024), ind(R("mt"), R("ln", l0, l0 + 64)), bias=1.0, scale=0.25)
-        o = R(("pC", "pD")[st], 64 * c, 64 * c + 64)
-        mm(o, [(o[0], T.mcb[:, 15 - i:143 - i], T.wr[:, b + i:b + 1024:16], i == 0, i == 15) for i in range(16)], [R("wr", b, b + 1024), R("mcb")])
+        w, src, sc = R("wr", b, b + 1024), ind(R("mt"), R("ln", l0, l0 + 64)), (-1.0, -1.0 / BIG)[st]
+        if q == "s":
+            act(w, src, scale=sc)
+        else:
+            ts(w, src, A.mult, sc)
+        o = R(("pC", "pE")[st], 64 * c, 64 * c + 64)
+        mm(o, [(o[0], T.mid[:], T.jh[:, 64 * c:64 * c + 64], True, False)] * (1 - st) +
+           [(o[0], T.mcb[:, 15 - i:143 - i], T.wr[:, b + i:b + 1024:16], st == 1 and i == 0, i == 15) for i in range(16)], [w, R("mcb"), R("mid"), R("jh")])
 
     def colour(st, x0, x1):
         b = 2048 * st
-        act(R("eg", b + x0, b + x1), ind(R("et"), R("oe", (b + x0) // 16, (b + x1) // 16)), bias=-0.375, scale=-0.25)
+        win = R("B", ET, R2 + x1) if st else R("B", R1, R2)
+        act(R("eg", b + x0, b + x1), ind(win, R("oe", (b + x0) // 16, (b + x1) // 16)), bias=-0.375, scale=-0.25)
 
-    def colour_list(st, f):
-        c = 128 * st
-        tt(R("ft", c, c + 128), R("zf", c, c + 128), f, A.mult)
-        ts(R("oe", c, c + 128), R("ft", c, c + 128), A.add, 4096.0)
+    def five(q, st, x0, x1):
+        x, z = R("B", (R1, R2)[st] + x0, (R1, R2)[st] + x1), R("pA", x0, x1)
+        if q == "s":
+            act(z, x, scale=1.25)
+        else:
+            ts(z, x, A.mult, 1.25)
 
-    def step(st, x0, x1):
-        x, m, y = R("xw", x0, x1), R("pA", x0, x1), R("xi", x0, x1)
-        if st == 1:
-            for b in range(x0 // 512, x1 // 512):
-                mm(R("pA", 512 * b, 512 * b + 512), [(T.pA[:, 512 * b + i:512 * b + 512:16], T.mex[:, 128 * i:128 * i + 128], T.m2[:, 32 * b:32 * b + 32], True, True)
-                                                     for i in range(16)], [R("mex"), R("m2")])
-            tt(m, x, m, A.mult)
-        tt(y, R("eg", 2048 * st + x0, 2048 * st + x1), m, A.add)
-        ts(x, y, A.max, 0.0, A.min, float(TOP))
+    def step(st, x0, x1, out):
+        y = R("xi", x0, x1)
+        tt(y, R("eg", 2048 * st + x0, 2048 * st + x1), R("pA", x0, x1), A.add)
+        ts(out, y, A.max, 0.0, A.min, float(TOP))
 
     KEEP = (4, 2, 0)
+
+    def differences(t):
+        w, n = 128 * (KEEP[t] + 1), ("la", "lb")[t]
+        tt(R("dd", 0, w), R(n, 128, 128 + w), R(n, 0, w), A.subtract)
+
+    def behind(t):
+        if t == 0:
+            place_lists(at(1, 0, 2))
+            differences(1)
+        else:
+            dma("y", [(T.lq[rows(o), :, j, :], T.lz[rows(a), :, o, :]) for o in four for j, a in enumerate(order)], [("lz", 0, 3)], [("lq", 0, 1 << 20)])
+            dma("y", [(T.B[rows(o), R1 + 512 * j:R1 + 512 * j + 512], T.B[rows(a), 512 * o:512 * o + 512]) for o in four for j, a in enumerate(order)],
+                [("B", 0, 2048)], [("B", R1, R1 + 2048)])
+
     for t in range(3):
         last = t == 2
-        old, new = L[t % 2], L[1 - t % 2]
-        late = [j for j in range(4) if 3 * j + 3 > 12 - VSHARE]
-        for h in range(2):
-            for j in range(4):
-                look_w(t, h, [k for k in range(3 * j, 3 * j + 3) if h == 0 or k < 12 - VSHARE], "s")
-                if h == 0 or j not in late:
-                    list_form(h, j)
+        lists(t, 0)
         if t == 0:
-            prepx(0)
-            consts()
-            cp(R("xw", 0, 1024), R("xi", 0, 1024))
-            spread("xw", 0, 1024, 2048)
-            cp(R("xw", 1024, 2048), R("xi", 1024, 2048))
-            spread("xw", 1024, 1024, 2048)
-            dma("y", [(T.thi[rows(s, o), :], T.thl[mine(s), o:o + 1]) for s, o in SO], [("thl", 0, 4)], [("thi", 0, 1)])
-            for u in (1, 2):
-                fetch(u, "y")
-                stage(u, "y")
-                dma("y", [(CG[u][:, own], T.sc[4 * u + me])], [("sc", u, u + 1)], [("cg%d" % u, 0, 768)])
-                send("r_c%d" % u, ("sc", u, u + 1), lambda k: T.sc[4 * u + k], CG[u][:, own])
-                rwait("cg%d" % u, 0, 768, "r_c%d" % u)
+            prep(2)
+        if FOLD:
+            for a in [FOLD] + list(range(FOLD)):
+                gather_x(t, 0, a)
+            fold(t)
+            if t:
+                run(look("v", t, 1, 2))
+                run(look("v", t, 1, 3))
+            minmax(0, FOLD)
+            lists(t, 1)
+            for a in range(FOLD + 1, 4):
+                gather_x(t, 0, a)
+                minmax(0, a)
         else:
-            for k in range(1, KEEP[t - 1]):
-                place(k, new, old)
-            cursors()
-            place_lists(old)
-        for _ in lists(t, 0):
-            pass
-        look_w(t, 1, range(12 - VSHARE, 12), "v")
-        for j in late:
-            list_form(1, j)
-        gen = lists(t, 1)
-        for k in range(12):
-            gather_x(0, k)
-            minmax(0, k)
-            if k > 2:
-                next(gen, None)
-                next(gen, None)
-        for _ in gen:
-            pass
-        if t == 0:
-            cp(R("thf"), R("thi"))
-        if not last:
-            w = 128 * (KEEP[t] + 1)
-            tt(R("dd", 0, w), R(old, 128, 128 + w), R(old, 0, w), A.subtract)
-        spread("et", 0, 512, 1024)
-        for k in range(12):
-            gather_x(1, k)
-            if k == 2:
+            for a in four:
+                gather_x(t, 0, a)
+                if t and a < 2:
+                    run(look("s", t, 1, 2 + a))
+                if a == 2:
+                    lists(t, 1)
+                minmax(0, a)
+            spread(ET, ET, 0, 512, 1024)
+        if t:
+            behind(t - 1)
+        else:
+            dma("y", [(T.xi[rows(a), 1024:1792], T.ray[rows(me), :] if a == me else T.lr[a]) for a in four], [("lr", 0, 4)], [("xi", 1024, 1792)])
+            later()
+            op("v", lambda: g.vector.tensor_reduce(T.thf[:], T.er[:, 0:4, 96], X.X, A.add), [V(None, "er", 0, 400)], [R("thf")])
+        for a in four:
+            gather_x(t, 1, a)
+            if a == 1 and not FOLD:
                 flags(0)
-            minmax(1, k)
+            if a == 3 and FOLD:
+                merge()
+                spread(ET, ET, 0, 512, 1024)
+                flags(0)
+            minmax(1, a)
+            if a == 1 and t == 0:
+                cp(R("la"), R("xi", 1024, 1792))
+                differences(0)
+                place_lists(at(0, 0, 2))
+            if a == 1 and last:
+                place_lists(V(T.lq[:, 0:2], "lq"))
         flags(1)
         ts(R("odd"), R("pC", 0, 64), A.is_ge, 9.0)
         op("v", lambda: g.vector.tensor_tensor_scan(T.cu[:, 16:80], T.odd[:], T.zz[:], 0.0, A.add, A.max), [R("odd"), R("zz")], [R("cu", 16, 80)])
-        mm(R("pD", 0, 1), [(T.pD[:, 0:1], T.mtri[:], T.cu[:, 79:80], True, True)], [R("cu", 16, 80), R("mtri")])
-        ts(R("cs", 15, 80), R("cu", 15, 80), A.add, R("pD", 0, 1), A.min, 256.0)
+        mm(R("pE", 0, 1), [(T.pE[:, 0:1], T.mtri[:], T.cu[:, 79:80], True, True)], [R("cu", 16, 80), R("mtri")])
+        ts(R("cs", 15, 80), R("cu", 15, 80), A.add, R("pE", 0, 1), A.min, 256.0)
         tt(R("cv"), R("cs", 16, 80), R("cs", 15, 79), A.subtract)
-        dma("ys", [(T.mt[64 * s + 16 * a:64 * s + 16 * a + 1, :], T.cv[64 * s:64 * s + 64, :]) for s, a in SO], [("cv", 0, 64)], [("mt", 0, 4096)])
-        spread("et", 512, 512, 1024)
-        if not last:
-            prep(t + 1, "pB")
-            prepx(t + 1)
-        ch = CHUNKS_END if last else CHUNKS
-        flag(0, 0)
-        flag(0, 1)
-        for b in range(0, 2048, 512):
-            o = R("pA", b, b + 512)
-            mm(o, [(o[0], T.mbc[:], T.wr[:, b:b + 512], True, True)], [R("wr", b, b + 512), R("mbc")])
-        flag(1, 0)
-        flag(1, 1)
-        ts(f1, R("pC", 0, 128), A.mult, -4.0, A.add, -4.0)
-        colour_list(0, f1)
-        for x0, x1 in ch:
-            tt(R("pA", x0, x1), R("xw", x0, x1), R("pA", x0, x1), A.mult)
-        ts(f2, f2, A.mult, -4.0, A.add, -4.0)
+        mm(R("pC", 256, 512), [(T.pC[:, 256 + 64 * j:320 + 64 * j], T.msel[:, 128 * j:128 * j + 128], T.cv[:], True, True) for j in four], [R("cv"), R("msel")])
+        cp(R("mp"), R("pC", 256, 512))
+        dma("y", [(T.mt[0:128:16, :], T.mp[:])], [("mp", 0, 256)], [("mt", 0, 4096)])
+        spread(ET, ET, 512, 512, 1024)
+        ch = [0, 512, 1024, 1536]
+        five("s", 0, 0, 1024)
+        five("s", 0, 1024, 2048)
+        for c in range(2):
+            flag("s", 0, c)
+            flag("v", 1, c)
+        tt(R("ft"), R("ce"), R("pC", 0, 128), A.min)
+        ts(f1, R("pC", 0, 128), A.is_ge, BIG / 2)
+        ts(R("oe", 0, 128), R("ft"), A.add, R("lanef"))
         tt(f2, f1, f2, A.mult)
-        colour_list(1, f2)
-        ts(R("m2"), f2, A.mult, 0.25, A.add, 1.0)
-        for c in ch:
-            colour(0, *c)
-            colour(1, *c)
-        if not last:
-            place(0, old, new)
-            table_w(new)
+        if last:
+            for c in ch:
+                colour(0, c, c + 512)
         else:
-            cursors()
+            colour(0, 0, 1024)
+            colour(0, 1024, 2048)
+            place(t, 0)
+            n = at(t + 1, 0)
+            mm(R("pC", 256, 384), [(T.pC[:, 256:384], T.mper[:], n[0], True, True)], [n, R("mper")])
+            cp(R("wp"), R("pC", 256, 384))
+            dma("y", [(T.wt[16 * j:16 * j + 1, :], T.wp[64 * (j % 2):64 * (j % 2) + 64, :]) for j in range(8)], [("wp", 0, 128)], [("wt", 0, 8192)])
+        tt(R("ft"), R("zf"), f2, A.mult)
+        tt(R("ft"), R("ft"), R("sj"), A.add)
+        cp(R("oe", 128, 256), R("ft"))
+        if last:
+            tt(R("cc"), V(T.lq[:, 2], "lq"), f1, A.add)
+            tt(R("cc"), R("cc"), f2, A.add)
             ts(R("cf"), R("cc"), A.min, 5.0)
-            dma("y", [(T.sy[a, 64 * s:64 * s + 64, :], T.cf[rows(s, a), :]) for s, a in SO if a != me], [("cf", 0, 128)], [("sy", 0, 4)])
-            dma("y", [(T.yc[mine(s), :], T.cf[rows(s, me), :]) for s in range(2)], [("cf", 0, 128)], [])
-            send("r_yc", ("sy", 0, 4), lambda k: T.sy[k], T.ly[me])
-            rwait("ly", 0, 4, "r_yc")
-        for x0, x1 in ch:
-            step(0, x0, x1)
-            step(1, x0, x1)
-            if not last:
-                spread("xw", x0, x1 - x0, 2048)
-            else:
-                c, x = x0 // 512, [("xw", x0, x1)]
-                dma("ys", [(T.so[4 * c + a, 64 * s:64 * s + 64, :], T.xw[rows(s, a), x0:x1]) for s, a in SO if a != me], x, [("so", 4 * c, 4 * c + 4)])
-                dma("y", [(T.yx[mine(s), x0:x1], T.xw[rows(s, me), x0:x1]) for s in range(2)], x, [])
-                send("r_x%d" % c, ("so", 4 * c, 4 * c + 4), lambda k: T.so[4 * c + k], T.lo[4 * c + me])
-                rwait("lo", 4 * c, 4 * c + 4, "r_x%d" % c)
+            send("r_yc", ("cf", 0, 128), lambda k: T.cf[:, 32 * order.index(k):32 * order.index(k) + 32], T.lc[me], ("lc", 0, 4), "l_end")
+            dma("y", [(T.yc[rows(me), 32 * o:32 * o + 32], T.cf[rows(o), 96:128]) for o in four], [("cf", 0, 128)], [])
+            dma("y", [(T.yc[rows(k), 32 * o:32 * o + 32], T.lc[k, rows(o), :]) for k in others for o in four], [("lc", 0, 4)], [])
+        base = (R1, S0)[t % 2]
 
-    dma("y", [(T.yc[32 * k:32 * k + 32, :], T.ly[k]) for k in others], [("ly", 0, 4)], [])
-    for c in range(4):
-        dma("ys", [(T.yx[32 * k:32 * k + 32, 512 * c:512 * c + 512], T.lo[4 * c + k]) for k in others], [("lo", 4 * c, 4 * c + 4)], [])
-    g.wait_ge(T.sem["r_loc"], nloc[0])
+        def second(c):
+            if not last:
+                step(1, c, c + 512, R("B", base + c, base + c + 512))
+                spread(base, 0, c, 512, 2048)
+                return
+            a = order[c // 512]
+            step(1, c, c + 512, R("eg", c, c + 512))
+            if a == me:
+                dma("s", [(T.yx[rows(me), 512 * o:512 * o + 512], T.eg[rows(o), c:c + 512]) for o in four], [("eg", c, c + 512)], [])
+                return
+            waits("g", "dma", [("eg", c, c + 512)], [])
+            es = eo if a in off else el
+            g.remote_dma_fused([transfer(a, es, "r_x%d" % me, T.eg[:, c:c + 512], T.ly[me])], local_sem=T.sem["l_end"])
+            nend[0] += len(es)
+            arrive(("ly", a, a + 1), "r_x%d" % a, len(es))
+
+        gen = iter(()) if last else (x for a in range(2) for x in look("ss", t + 1, 0, a))
+        for j, c in enumerate(ch):
+            step(0, c, c + 512, R("B", R2 + c, R2 + c + 512))
+            five("s" if last or j < FIVE else "v", 1, c, c + 512)
+            colour(1, c, c + 512)
+            if j:
+                second(ch[j - 1])
+                run(gen, 1)
+        second(ch[3])
+        if not last:
+            run(gen)
+            run(look("sv", t + 1, 0, 2))
+            run(look("sv", t + 1, 0, 3))
+            for k in range(1, KEEP[t]):
+                place(t, k)
+            tt(R("cc"), R("cc"), f1, A.add)
+            tt(R("cc") if t == 0 else V(T.lz[:, 2], "lz", 2, 3), R("cc"), f2, A.add)
+            run(look("s", t + 1, 1, 0))
+            run(look("s", t + 1, 1, 1))
+
+    turn = lambda k: [j for j in four if far(j, k)].index(me) if far(k, me) else 2
+    for j, k in enumerate(sorted(others, key=turn)):
+        dma("y" if j == 0 else "ys", [(T.yx[rows(k), 512 * o:512 * o + 512], T.ly[k, rows(o), :]) for o in four], [("ly", k, k + 1)], [])
+    for s in SENT:
+        g.wait_ge(T.sem[s], SENT[s])
+    g.wait_ge(T.sem["l_end"], nend[0])
     for s in sorted(allsem):
         wait("y", (s, allsem[s]))

@@ -13,22 +13,27 @@ def _buf(where, dtype, **shapes):
 
 S0, R1, ET, R2 = 0, 8192, 10240, 14336
 _buf("dram", "int32", sr=[4, 128, 192], lr=[4, 128, 192])
-_buf("dram", "float32", lp=[8, 128, 256], ly=[4, 128, 512], lc=[4, 128, 32])
-_buf("sbuf", "int32", cq=[128, 36, 2, 32], xi=2048, tho=1, zi=256, it0=144, it1=144, vci=96, pc=1, lane=1, grp=1, oi=1, ji=128, ip=128, iq=128)
+_buf("dram", "float32", lp=[8, 128, 256], ly=[4, 128, 544])
+_buf("sbuf", "int32", cq=[128, 36, 2, 32], xi=2048, la=768, xbt=1536, xbr=[128, 4, 6, 64], cxi=8, tho=1, zi=256, it0=144, it1=144, vci=96, pc=1, lane=1, grp=1, oi=1, ji=128, iq=128)
 _buf("sbuf", "uint16", lw0=[128, 8, 96], lws=[128, 4, 12, 32], lwt=1536, lwr=[128, 4, 384], lx=768, ln=256, oe=256)
-_buf("sbuf", "bfloat16", wr=6144, mt=4096, fl=1024, mcb=144, mid=128, mb2=144, vct=96, jh=128, cv=64, msel=512, mp=256)
+_buf("sbuf", "bfloat16", wr=6144, mt=4096, fl=1024, mcb=144, mid=128, mb2=144, vct=96, jh=128, cv=64, msel=512, mp=256, mw=512, wh=256)
 _buf("sbuf", "float32", B=16384, wt=8192, xg=6144, eg=4096, es=[128, 8, 100], el=800, er=[128, 8, 100],
-     xbs=[128, 4, 12, 32], xbr=[128, 4, 384], le=384, l1=192, l2=96, l3=32, lm=96, le2=384, thf=1, odd=64, zz=64, cu=80, cs=80,
-     la=768, lb=512, lz=[128, 3, 4, 32], lq=[128, 3, 4, 32], dd=640, ce=128, zf=128, sj=128, f1=128, ft=128, fu=128, cc=128, cf=128, wp=128,
-     lanef=1, grpf=1, of=1, k0=1, nk0=1, g16=1, nb=2, pb=2, cole=1, col1=1, mtri=128, mper=128)
+     colx=8, le=384, l1=192, l2=96, l3=32, lm=96, le2=384, thf=1, odd=64, zz=64, cu=80, cs=80,
+     lb=512, lz=[128, 3, 4, 32], lq=[128, 3, 4, 32], dd=640, ce=128, zf=128, sj=128, f1=128, ft=128, fu=128, cc=128,
+     lanef=1, grpf=1, of=1, k0=1, nk0=1, g16=1, nb=2, pb=2, cole=1, col1=1, isa=4, mtri=128)
 _buf("psum", "float32", pA=2048, pD=1024, pC=512, pE=512)
 PSUM = ("pA", "pD", "pC", "pE")
 ENG = {"v": "q_v", "s": "q_s", "t": "q_t", "g": "q_g"}
 DSEM = ["d%d" % j for j in range(100)]
-SEMAPHORES = list(ENG.values()) + DSEM + ["r_p0", "r_p1", "r_e0", "r_e1", "r_ray", "r_lw", "r_xb", "r_yc", "r_x0", "r_x1", "r_x2", "r_x3",
+SEMAPHORES = list(ENG.values()) + DSEM + ["r_p0", "r_p1", "r_q0", "r_q1", "r_e0", "r_e1", "r_ray", "r_lw", "r_xb", "r_x0", "r_x1", "r_x2", "r_x3",
                                           "r_f0", "r_f1", "r_f2", "l_px", "l_list", "l_end"]
 FIVE = 2
-FOLD = 2
+FIRST = 0
+INIT = "ssssss"
+FS = 32
+VX = (2, 4, 4)
+SPREAD = ((0, 1024), (1024, 2048))
+FOLD = (6, 7, 7)
 
 
 def helper(core, T, topo):
@@ -44,7 +49,7 @@ def rank_program(g, core, T, topo):
     me = T.rank_of(core)
     if me is None:
         for c in T.cores:
-            if FOLD and helper(c, T, topo) == core:
+            if helper(c, T, topo) == core:
                 rid, pid, _se = topo.addr(c)
                 es = topo.engines(core, c)
                 for t in range(3):
@@ -161,7 +166,8 @@ def rank_program(g, core, T, topo):
 
     others = [k for k in range(4) if k != me]
     far = lambda a, b: topo.chip(T.cores[a]) != topo.chip(T.cores[b])
-    off = [k for k in others if far(k, me)]
+    away = lambda a: sorted((k for k in range(4) if far(k, a)), key=lambda k: topo.die(T.cores[k]) != topo.die(T.cores[a]))
+    off = away(me)
     on = [k for k in others if k not in off]
     eo = topo.engines(core, T.cores[off[0]])
     el = [e for e in topo.engines(core, T.cores[on[0]]) if e not in eo]
@@ -198,51 +204,53 @@ def rank_program(g, core, T, topo):
     dma("s", [(T.zi[:, 0:128], T.ray[:, 0:128])], [], [("zi", 0, 128)])
     dma("s", [(T.cq[:, 0:12], T.cand[:, 0:768])], [], [("cq", 0, 768)])
     for hf in range(2):
-        dma("ys"[hf], [(T.xi[:, 1024 * hf + 256 * k:1024 * hf + 256 * k + 256], T.px[rows(k), 1024 * hf:1024 * hf + 1024]) for k in order],
+        dma("y", [(T.xi[:, 1024 * hf + 256 * k:1024 * hf + 256 * k + 256], T.px[rows(k), 1024 * hf:1024 * hf + 1024]) for k in order],
             [], [("xi", 1024 * hf, 1024 * hf + 1024)])
     dma("s", [(T.tho[:], T.th[:])], [], [("tho", 0, 1)])
     for n, a, b, pat, base, cm in [("pc", 0, 1, [[0, 1]], 0, 1), ("it1", 0, 143, [[1, 143]], -15, -1), ("vci", 0, 96, [[0, 3], [16, 32]], -255, 0),
-                                   ("it0", 0, 143, [[1, 143]], 0, 0), ("ji", 0, 128, [[16, 128]], 0, 0), ("ip", 0, 128, [[16, 2], [32, 4], [1, 16]], 0, -1)] + [
+                                   ("it0", 0, 143, [[1, 143]], 0, 0), ("ji", 0, 128, [[16, 128]], 0, 0)] + [
                                    ("iq", 32 * o, 32 * o + 32, [[16, 2], [32, 4], [4, 4]], 0, -1) for o in four]:
         op("g", lambda: g.iota(T[n][:, a:b], pat, base, cm), [], [R(n, a, b)])
     fill(R("wt", 0, 2048), 0.0)
     ts(R("lane"), R("pc"), A.bitwise_and, 15)
-    fill(V(T.es[:], "es"), 0.0)
+    fill(V(T.es[:, :, 96:100], "es"), 0.0)
     cp(R("lanef"), R("lane"))
     ts(R("k0"), R("lane"), A.is_equal, 0)
     cp(R("lb", 0, 128), R("zi", 0, 128))
     dma("y", [(T.wt[0:128:16, 0:2048], T.lb[:, 0:128])], [("lb", 0, 128)], [("wt", 0, 2048)])
+    dma("y", [(T.cq[:, 12:36], T.cand[:, 768:2304])], [], [("cq", 768, 2304)])
     ts(R("nk0"), R("k0"), A.mult, -BIG)
 
     def pixels(hf):
         c = 2048 + 1024 * hf
         cp(R("eg", c, c + 1024), R("xi", c - 2048, c - 1024))
-        send("r_p%d" % hf, ("eg", c, c + 1024), lambda k: T.eg[:, c + 256 * k:c + 256 * k + 256], T.lp[4 * hf + me], ("lp", 4 * hf, 4 * hf + 4), "l_px")
+        waits("g", "dma", [("eg", c, c + 1024)], [])
+        sem = lambda k: ("r_p%d" if k in off else "r_q%d") % hf
+        g.remote_dma_fused([transfer(k, eng[k], sem(k), T.eg[:, c + 256 * k:c + 256 * k + 256], T.lp[4 * hf + me]) for k in others], local_sem=T.sem["l_px"])
+        hist["eg"].append((c, c + 1024, False, "remote", ("l_px", SENT["l_px"])))
+        for k in others:
+            arrive(("lp", 4 * hf + k, 4 * hf + k + 1), sem(k), len(eo) if k in off else len(el))
 
     def table_x(q, hf, who):
         c = 1024 * hf
         src = lambda a: T.eg[:, 2048 + c + 256 * a:2048 + c + 256 * a + 256] if a == me else T.lp[4 * hf + a]
         col = lambda a, o: 2048 + 2048 * ((a - o - 1) % 4) + c
         dma(q, [(T.B[rows(o), col(a, o):col(a, o) + 1024], src(a)) for a in who for o in four],
-            [("eg", 2048 + c, 3072 + c) if who == [me] else ("lp", 4 * hf, 4 * hf + 4)], [("B", 2048 * d + c, 2048 * d + c + 1024) for d in (1, 2, 3, 4)], apart=True)
+            [("eg", 2048 + c, 3072 + c) if a == me else ("lp", 4 * hf + a, 4 * hf + a + 1) for a in who], [("B", 2048 * d + c, 2048 * d + c + 1024) for d in (1, 2, 3, 4)], apart=True)
 
-    def places(c, n, outs, add):
+    def places(c, n, outs, lane, add):
         p = R("pA", 1024, 1024 + n)
         ts(R("xi", 0, n), c, A.bitwise_and, 15)
-        ts(p, R("xi", 0, n), A.mult, 2047.0)
+        ts(p, R("xi", 0, n), A.mult, 16.0 * lane - 1)
         tt(p, c, p, A.add)
         for m in range(3):
             ts(outs(m), R("pA", 1024 + m * n // 3, 1024 + (m + 1) * n // 3), A.mult, 0.0625, A.add, add)
 
     def prep0(h):
-        places(V(T.cq[:, 0:12, h, :], "cq", 0, 768), 384, lambda m: V(T.lw0[:, 4 * h:4 * h + 4, 32 * m:32 * m + 32], "lw0", h, h + 1), 0.0)
+        places(V(T.cq[:, 0:12, h, :], "cq", 0, 768), 384, lambda m: V(T.lw0[:, 4 * h:4 * h + 4, 32 * m:32 * m + 32], "lw0", h, h + 1), 128, 0.0)
 
     def prep(t):
-        places(V(T.cq[:, 12 * t:12 * t + 12], "cq", 768 * t, 768 * t + 768), 768, lambda m: V(T.lws[:, :, 6 * t - 6 + m:6 * t:3, :], "lws"), 2048.0 * me)
-        for o in four:
-            fill(R("pC", 64 * o, 64 * o + 64), 2048.0 * ((me - o - 2 + t) % 4))
-        for m in range(3):
-            tt(V(T.xbs[:, :, 6 * t - 6 + m:6 * t:3, :], "xbs"), V(T.cq[:, 12 * t + 4 * m:12 * t + 4 * m + 4], "cq", 768 * t, 768 * t + 768), R("pC", 0, 256), A.add)
+        places(V(T.cq[:, 12 * t:12 * t + 12], "cq", 768 * t, 768 * t + 768), 768, lambda m: V(T.lws[:, :, 6 * t - 6 + m:6 * t:3, :], "lws"), 512, 128.0 * me)
 
     nw = [0]
 
@@ -264,7 +272,7 @@ def rank_program(g, core, T, topo):
         b = 1024.0 * o + 512.0 * h + 255.0
         run(look_w(qs, R("wt", 0, 2048), lambda u, v: V(T.lw0[:, 4 * h + o, u:v], "lw0", h, h + 1), -b, b, R(("pA", "pE")[h], 96 * o, 96 * o + 96)))
 
-    def seen0(h):
+    def seen0(h, qs):
         for o in four:
             p = R(("pA", "pE")[h], 96 * o, 96 * o + 96)
             ts(p, p, A.max, 0.0, A.subtract, 2048.0 * ((me - o - 1) % 4))
@@ -272,8 +280,11 @@ def rank_program(g, core, T, topo):
             c = 400 * h + 100 * o
             tt(V(T.es[:, 4 * h + o, 0:96], "es", c, c + 96), V(T.cq[:, o:12:4, h, :], "cq", 0, 768), R(("pA", "pE")[h], 96 * o, 96 * o + 96), A.subtract)
         c = 400 * h
-        dma("y", [(T.el[rows(o), c + 100 * k:c + 100 * k + 100], T.es[rows(k), 4 * h + o, :]) for k in others for o in four], [("es", c, c + 400)], [("el", c, c + 400)])
+        dma(qs, [(T.el[rows(o), c + 100 * k:c + 100 * k + 100], T.es[rows(k), 4 * h + o, :]) for k in others for o in four], [("es", c, c + 400)], [("el", c, c + 400)])
         send("r_e%d" % h, ("el", c, c + 400), lambda k: T.el[:, c + 100 * k:c + 100 * k + 100], T.er[:, 4 * h + me, :], ("er", c, c + 400), "l_list")
+
+    def seen_own(h):
+        c = 400 * h
         dma("y", [(T.er[rows(o), 4 * h + me, :], T.es[rows(me), 4 * h + o, :]) for o in four], [("es", c, c + 400)], [("er", c, c + 400)], apart=True)
 
     def consts():
@@ -287,6 +298,10 @@ def rank_program(g, core, T, topo):
             ts(R("nb", h, h + 1), R("of"), A.mult, -1024.0, A.add, -(512.0 * h + 255.0))
             ts(R("pb", h, h + 1), R("of"), A.mult, 1024.0, A.add, 512.0 * h + 255.0)
         ts(R("cole"), R("of"), A.mult, -1024.0, A.add, 4096.0)
+        ts(R("cxi", 0, 4), R("it0", 3, 7), A.subtract, R("of"))
+        ts(R("cxi", 4, 8), R("it0", 4, 8), A.subtract, R("of"))
+        ts(R("cxi"), R("cxi"), A.bitwise_and, 3)
+        ts(R("colx"), R("cxi"), A.mult, 2048.0)
         ts(R("col1"), R("lanef"), A.mult, -1.0, A.add, 2048.0)
         ts(R("mb2", 0, 143), R("it0", 0, 143), A.subtract, R("g16"), A.is_equal, 0.0)
         ts(R("fu"), R("it1", 15, 143), A.is_gt, 0)
@@ -294,18 +309,21 @@ def rank_program(g, core, T, topo):
         cp(R("jh"), R("ji"))
         ts(R("sj"), R("ji"), A.add, R("lanef"), A.add, 4096.0)
         tt(R("mtri"), R("f1"), R("fu"), A.mult)
-        ts(R("mper"), R("ip"), A.is_equal, 0)
+        yield
+        ts(R("zi", 128, 256), R("it1", 15, 143), A.bitwise_and, 31)
         for j in four:
+            ts(R("isa", j, j + 1), R("of"), A.is_equal, float(j))
+        for j in four:
+            ts(R("mw", 128 * j, 128 * j + 128), R("zi", 128, 256), A.is_equal, 0, A.mult, R("isa", j, j + 1))
             ts(R("msel", 128 * j, 128 * j + 128), R("iq"), A.is_equal, -j)
         fill(R("zz"), 0.0)
         fill(R("cu", 0, 16), 0.0)
         fill(R("cc"), 0.0)
 
-    def later():
-        for src, sn, til, tn, c, lan, ln, sem in ((T.lws, "lws", T.lwt, "lwt", 0, T.lwr, "lwr", "r_lw"), (T.xbs, "xbs", T.wt, "wt", 2048, T.xbr, "xbr", "r_xb")):
-            dma("y", [(lan[rows(o), k, :] if k == me else til[rows(o), c + 384 * k:c + 384 * k + 384], src[rows(k), o]) for k in order for o in four],
-                [(sn, 0, 1 << 20)], [(tn, c, c + 1536), (ln, 0, 1536)])
-            send(sem, (tn, c, c + 1536), lambda k: til[:, c + 384 * k:c + 384 * k + 384], lan[:, me, :], (ln, 0, 1536), "l_list")
+    def later(src, need, tn, ln, sem):
+        til, lan = T[tn], T[ln]
+        dma("y", [(lan[rows(o), k] if k == me else til[rows(o), 384 * k:384 * k + 384], src(k, o)) for k in order for o in four], [need], [(tn, 0, 1536), (ln, 0, 1536)])
+        send(sem, (tn, 0, 1536), lambda k: til[:, 384 * k:384 * k + 384], lan[:, me], (ln, 0, 1536), "l_list")
 
     pixels(0)
     ts(R("mcb", 0, 143), R("it1", 0, 143), A.is_equal, 0, A.mult, R("nk0"))
@@ -313,28 +331,29 @@ def rank_program(g, core, T, topo):
     ts(R("mid"), R("it1", 15, 143), A.is_equal, 0)
     ts(R("vct"), R("vci"), A.add, R("lanef"), A.mult, BIG)
     look0("s", 0, 0)
-    look0("v", 0, 3)
     pixels(1)
     table_x("y", 0, [me])
     table_x("y", 1, [me])
-    dma("y", [(T.cq[:, 12:36], T.cand[:, 768:2304])], [], [("cq", 768, 2304)])
     cp(V(T.es[:, me, 96:97], "es", 100 * me + 96, 100 * me + 97), R("tho"))
     look0("s", 0, 1)
-    look0("sv", 0, 2)
+    look0("v", 0, 3)
     prep0(1)
-    fill(R("mt"), 0.0)
-    seen0(0)
-    table_x("y", 0, others)
-    table_x("y", 1, others)
-    for o in four:
-        look0("s", 1, o)
-    for c in (2048, 4096, 6144):
-        act(R("wt", c, c + 2048), R("wt", 0, 2048))
-    consts()
+    look0("s", 0, 2)
+    look0("s", 1, 0)
+    table_x("y", 0, on)
+    table_x("y", 1, on)
+    gen = consts()
+    run(gen, 1)
+    seen0(0, "y")
+    run(gen)
+    seen_own(0)
+    table_x("y", 0, off)
+    table_x("y", 1, off)
+    look0("s", 1, 1)
+    look0("s", 1, 2)
+    look0("s", 1, 3)
     prep(1)
-    seen0(1)
     dma("y", [(T.sr[:], T.ray[:])], [], [("sr", 0, 4)])
-    send("r_ray", ("sr", 0, 4), lambda k: T.sr[k], T.lr[me], ("lr", 0, 4), "l_list")
 
     def look(qs, t, h, a):
         c = 192 * (t - 1) + 96 * h
@@ -346,9 +365,11 @@ def rank_program(g, core, T, topo):
             E = lambda a, b: V(T.er[:, 4 * h + a:4 * h + b, 0:96], "er", 400 * h, 400 * h + 400)
             ts(p, E(0, 4), A.mult, -1.0)
         else:
-            E, c = (lambda a, b: R("le", 96 * a, 96 * b)), 192 * (t - 1) + 96 * h
-            ts(p, p, A.max, 0.0)
-            tt(E(0, 4), V(T.xbr[:, :, c:c + 96], "xbr"), p, A.subtract)
+            E = lambda a, b: R("le", 96 * a, 96 * b)
+            for a in four:
+                q = R("pD", 512 * h + 96 * a, 512 * h + 96 * a + 96)
+                ts(q, q, A.max, 0.0, A.subtract, R("colx", 4 * t - 4 + a, 4 * t - 3 + a))
+            tt(E(0, 4), V(T.xbr[:, :, 3 * t - 3:3 * t, 32 * h:32 * h + 32], "xbr"), p, A.subtract)
         tt(R("l1"), E(0, 2), E(2, 4), A.max)
         tt(R("l2"), R("l1", 0, 96), R("l1", 96, 192), A.max)
         tt(R("l3"), R("l2", 0, 32), R("l2", 32, 64), A.max)
@@ -363,40 +384,45 @@ def rank_program(g, core, T, topo):
     def acc(h):
         return R("pA", 1024 * h, 1024 * h + 512), R("pA", 1024 * h + 512, 1024 * h + 1024)
 
-    first = lambda h: 0 if h else FOLD
+    first = lambda t, h: 0 if h else FOLD[t]
 
-    def pix(h, a, m, n):
-        return R("eg" if a < first(h) else "xg", 1536 * a + 512 * m, 1536 * a + 512 * n)
+    def pix(t, h, k, n):
+        return R("eg" if k < first(t, h) else "xg", 512 * k, 512 * n)
 
-    def gather_x(t, h, a):
-        c, w = 384 * h + 96 * a, (0 if t == 2 else 2048)
-        parts = ((0, 1), (1, 2), (2, 3)) if (h, a) in ((0, first(0)), (1, 3)) else ((0, 1), (1, 3)) if a == first(h) else ((0, 3),)
-        for m, n in parts:
-            act(pix(h, a, m, n), ind(R("B", w, w + 8192), R("lx", c + 32 * m, c + 32 * n)))
-            if a == first(h) and m == 0:
-                act(acc(h)[1], pix(h, a, 0, 1))
+    def gather_x(q, t, h, k, n):
+        w = 0 if t == 2 else 2048
+        src = ind(R("B", w, w + 8192), R("lx", 384 * h + 32 * k, 384 * h + 32 * n))
+        if q == "v":
+            cp(pix(t, h, k, n), src)
+        else:
+            act(pix(t, h, k, n), src)
+        if k == first(t, h):
+            if "v" != INIT[2 * t + h]:
+                act(acc(h)[1], pix(t, h, k, k + 1))
 
-    def minmax(h, a):
+    def minmax(t, h, k0, n):
         lo, hi = acc(h)
-        for m in range(3):
-            k = 3 * (a - first(h)) + m
-            if k:
-                done = (a, m) == (3, 2) and not first(h)
-                tt(R("B", ET + 512 * h, ET + 512 * h + 512) if done else lo, pix(h, a, m, m + 1), hi if k == 1 else lo, A.min)
-                tt(hi, pix(h, a, m, m + 1), hi, A.max)
+        for k in range(max(k0, first(t, h) + 1), n):
+            x = pix(t, h, k, k + 1)
+            if k == first(t, h) + 1 and "v" == INIT[2 * t + h]:
+                cp(hi, pix(t, h, k - 1, k))
+            tt(R("B", ET + 512, ET + 1024) if (h, k) == (1, 11) else lo, x, hi if k == first(t, h) + 1 else lo, A.min)
+            tt(hi, x, hi, A.max)
 
     def fold(t):
         c = helper(core, T, topo)
         rid, pid, _se = topo.addr(c)
         es = topo.engines(core, c)
         n = len(es) // 2
-        waits("g", "dma", [("eg", 0, 1536 * FOLD)], [("B", R2 + 1024, R2 + 2048)])
+        srcs = [pix(t, 0, k, k + 1) for k in range(FOLD[t])]
+        waits("g", "dma", [v[1][0] for v in srcs], [("B", R2 + 1024, R2 + 2048)])
         g.remote_dma_fused([RemoteDMATransfer(dst_ids=[DstId(rid=rid, pnc=pid)], dma_engine_mask=mask(es[j * n:j * n + n]), remote_sem=T.sem["r_f%d" % t],
-                                              srcs=[T.eg[:, 512 * k:512 * k + 512] for k in range(3 * FOLD)],
+                                              srcs=[v[0] for v in srcs],
                                               dsts=[T.xg[:, 1024 * t + 512 * j:1024 * t + 512 * j + 512]], alu_op=(3, 2)[j]) for j in range(2)], local_sem=T.sem["l_end"])
         nend[0] += 2 * n
         back = len(topo.engines(c, core))
-        hist["eg"].append((0, 1536 * FOLD, False, "remote", ("r_f%d" % t, back)))
+        for v in srcs:
+            hist[v[1][0][0]].append(v[1][0][1:] + (False, "remote", ("r_f%d" % t, back)))
         arrive(("B", R2 + 1024, R2 + 2048), "r_f%d" % t, back)
 
     def merge():
@@ -409,7 +435,7 @@ def rank_program(g, core, T, topo):
         lt, fl = R("B", R2 + c, R2 + c + 512), R("fl", c, c + 512)
         act(lt, R("B", ET + c, ET + c + 512), bias=R("thf"))
         tt(fl, acc(h)[1], lt, A.is_gt)
-        mm(R("pC", 0, 64), [(T.pC[:, 0:64], T.mb2[:, 15 - i:143 - i], T.fl[:, 64 * i:64 * i + 64], i == 0, i == 15) for i in range(8 * h, 8 * h + 8)], [fl, R("mb2")])
+        mm(R("pC", 0, 64), [(T.pC[:, 0:64], T.mb2[:, 15 - i:143 - i], T.fl[:, 64 * i:64 * i + 64], i == 8, i == 7) for i in range(8 * h, 8 * h + 8)], [fl, R("mb2")])
 
     def spread(src, dst, lo, w, width):
         items = []
@@ -425,29 +451,37 @@ def rank_program(g, core, T, topo):
         return V(T.lz[:, k:k + n], "lz", k, k + n)
 
     def place_lists(src):
-        cp(R("ln"), src)
-        ts(R("zi"), src, A.add, R("cole"))
-        ts(R("zi"), R("zi"), A.bitwise_and, 4095)
-        ts(R("ce"), R("zi", 0, 128), A.add, R("col1"))
-        tt(R("zf"), R("zi", 128, 256), R("sj"), A.subtract)
+        yield cp(R("ln"), src)
+        yield ts(R("zi"), src, A.add, R("cole"))
+        yield ts(R("zi"), R("zi"), A.bitwise_and, 4095)
+        yield ts(R("ce"), R("zi", 0, 128), A.add, R("col1"))
+        yield tt(R("zf"), R("zi", 128, 256), R("sj"), A.subtract)
 
     f1, f2 = R("f1"), R("pE", 0, 128)
 
     def place(t, k):
         c = 128 * k
-        tt(R("fu"), R("dd", c, c + 128), f1, A.mult)
-        tt(R("pE", 128, 256), R("dd", c + 128, c + 256), f2, A.mult)
-        tt(R("fu"), R("fu"), at(t, k), A.add)
+        tt(R("pE", 128, 256), R("dd", c, c + 128), R("pC", 128, 256), A.mult)
+        tt(R("fu"), R("dd", c + 128, c + 256), f2, A.mult)
+        tt(R("pE", 128, 256), at(t, k), R("pE", 128, 256), A.add)
         tt(at(t + 1, k), R("fu"), R("pE", 128, 256), A.add)
 
-    def flag(q, st, c):
+    def first_list(y, a, b):
+        tt(R("ft", a, b), R("ce", a, b), y, A.min)
+        ts(R("oe", a, b), R("ft", a, b), A.add, R("lanef"))
+        ts(R("f1", a, b), y, A.is_ge, BIG / 2)
+
+    def second_list(f, a, b):
+        tt(R("pE", 256 + a, 256 + b), R("zf", a, b), f, A.mult)
+        tt(R("ft", a, b), R("sj", a, b), R("pE", 256 + a, 256 + b), A.add)
+        cp(R("oe", 128 + a, 128 + b), R("ft", a, b))
+
+    def flag(st, c, o):
         b, l0 = 2048 * st + 1024 * c, 128 * st + 64 * c
-        w, src, sc = R("wr", b, b + 1024), ind(R("mt"), R("ln", l0, l0 + 64)), (-1.0, -1.0 / BIG)[st]
-        if q == "s":
-            act(w, src, scale=sc)
-        else:
-            ts(w, src, A.mult, sc)
-        o = R(("pC", "pE")[st], 64 * c, 64 * c + 64)
+        w, sc = R("wr", b, b + 1024), (-1.0, -1.0 / BIG)[st]
+        act(R("wr", b, b + 16 * FS), ind(R("mt"), R("ln", l0, l0 + FS)), scale=sc)
+        if FS < 64:
+            ts(R("wr", b + 16 * FS, b + 1024), ind(R("mt"), R("ln", l0 + FS, l0 + 64)), A.mult, sc)
         mm(o, [(o[0], T.mid[:], T.jh[:, 64 * c:64 * c + 64], True, False)] * (1 - st) +
            [(o[0], T.mcb[:, 15 - i:143 - i], T.wr[:, b + i:b + 1024:16], st == 1 and i == 0, i == 15) for i in range(16)], [w, R("mcb"), R("mid"), R("jh")])
 
@@ -470,148 +504,187 @@ def rank_program(g, core, T, topo):
 
     KEEP = (4, 2, 0)
 
-    def differences(t):
-        w, n = 128 * (KEEP[t] + 1), ("la", "lb")[t]
-        tt(R("dd", 0, w), R(n, 128, 128 + w), R(n, 0, w), A.subtract)
+    def differences(t, a, b):
+        n = ("la", "lb")[t]
+        tt(R("dd", 128 * a, 128 * b), R(n, 128 * a + 128, 128 * b + 128), R(n, 128 * a, 128 * b), A.subtract)
 
-    def behind(t):
-        if t == 0:
-            place_lists(at(1, 0, 2))
-            differences(1)
-        else:
-            dma("y", [(T.lq[rows(o), :, j, :], T.lz[rows(a), :, o, :]) for o in four for j, a in enumerate(order)], [("lz", 0, 3)], [("lq", 0, 1 << 20)])
-            dma("y", [(T.B[rows(o), R1 + 512 * j:R1 + 512 * j + 512], T.B[rows(a), 512 * o:512 * o + 512]) for o in four for j, a in enumerate(order)],
-                [("B", 0, 2048)], [("B", R1, R1 + 2048)])
+    def regroup():
+        dma("y", [(T.lq[rows(o), :, j, :], T.lz[rows(a), :, o, :]) for o in four for j, a in enumerate(order)], [("lz", 0, 3)], [("lq", 0, 1 << 20)])
+        dma("y", [(T.B[rows(o), R1 + 512 * j:R1 + 512 * j + 512], T.B[rows(a), 512 * o:512 * o + 512]) for o in four for j, a in enumerate(order)],
+            [("B", 0, 2048)], [("B", R1, R1 + 2048)])
 
     for t in range(3):
         last = t == 2
         lists(t, 0)
+        n = FOLD[t]
         if t == 0:
+            seen0(1, "y")
+            seen_own(1)
             prep(2)
-        if FOLD:
-            for a in [FOLD] + list(range(FOLD)):
-                gather_x(t, 0, a)
-            fold(t)
-            if t:
-                run(look("v", t, 1, 2))
-                run(look("v", t, 1, 3))
-            minmax(0, FOLD)
-            lists(t, 1)
-            for a in range(FOLD + 1, 4):
-                gather_x(t, 0, a)
-                minmax(0, a)
-        else:
-            for a in four:
-                gather_x(t, 0, a)
-                if t and a < 2:
-                    run(look("s", t, 1, 2 + a))
-                if a == 2:
-                    lists(t, 1)
-                minmax(0, a)
-            spread(ET, ET, 0, 512, 1024)
         if t:
-            behind(t - 1)
-        else:
-            dma("y", [(T.xi[rows(a), 1024:1792], T.ray[rows(me), :] if a == me else T.lr[a]) for a in four], [("lr", 0, 4)], [("xi", 1024, 1792)])
-            later()
+            run(look("v", t, 1, 3))
+        gather_x("s", t, 0, 0, n - VX[t])
+        if VX[t]:
+            gather_x("v", t, 0, n - VX[t], n)
+        fold(t)
+        if last:
+            regroup()
+        if t == 0:
+            send("r_ray", ("sr", 0, 4), lambda k: T.sr[k], T.lr[me], ("lr", 0, 4), "l_list")
+            op("g", lambda: g.iota(T.mt[:], [[0, 4096]], 0, 0, allow_small_or_imprecise_dtypes=True), [], [R("mt")])
+        for k0, k1 in ((n, n + 1), (n + 1, n + 2), (n + 2, 9), (9, 12)) if n < 7 else ((n, n + 1), (n + 1, n + 2), (n + 2, 12)):
+            gather_x("s", t, 0, k0, k1)
+        if t == 0:
+            waits("y", "dma", pix(t, 0, n + 1, n + 2)[1], [])
+            later(lambda k, o: T.lws[rows(k), o], ("lws", 0, 1 << 20), "lwt", "lwr", "r_lw")
+            later(lambda k, o: T.cq[rows(k), 12 + o:36:4], ("cq", 768, 2304), "xbt", "xbr", "r_xb")
+            op("g", lambda: g.iota(T.wt[:, 6144:8192], [[0, 2048]], 0, 0, allow_small_or_imprecise_dtypes=True), [], [R("wt", 6144, 8192)])
+        if t == 0:
+            minmax(t, 0, n, n + FIRST)
+        lists(t, 1)
+        if t == 1:
+            place(0, 2)
+            minmax(t, 0, n, n + 2)
+            place(0, 3)
+        minmax(t, 0, n + (FIRST, 2, 0)[t], 12)
+        if t == 0:
+            dma("y", [(T.la[rows(a), :], T.ray[rows(me), :] if a == me else T.lr[a]) for a in four], [("lr", 0, 4)], [("la", 0, 768)])
             op("v", lambda: g.vector.tensor_reduce(T.thf[:], T.er[:, 0:4, 96], X.X, A.add), [V(None, "er", 0, 400)], [R("thf")])
-        for a in four:
-            gather_x(t, 1, a)
-            if a == 1 and not FOLD:
-                flags(0)
-            if a == 3 and FOLD:
-                merge()
-                spread(ET, ET, 0, 512, 1024)
-                flags(0)
-            minmax(1, a)
-            if a == 1 and t == 0:
-                cp(R("la"), R("xi", 1024, 1792))
-                differences(0)
-                place_lists(at(0, 0, 2))
-            if a == 1 and last:
-                place_lists(V(T.lq[:, 0:2], "lq"))
+        for k0, k1 in ((0, 1), (1, 3), (3, 6), (6, 9), (9, 10), (10, 11), (11, 12)):
+            gather_x("s", t, 1, k0, k1)
+        for c in (2048, 4096) if t == 0 else ():
+            act(R("wt", c, c + 2048), R("wt", 0, 2048))
+        minmax(t, 1, 0, 12)
+        spread(ET, ET, 512, 512, 1024)
         flags(1)
+        merge()
+        flags(0)
+        gen = place_lists(V(T.lq[:, 0:2], "lq") if last else at(t, 0, 2))
+        run(gen, 2)
         ts(R("odd"), R("pC", 0, 64), A.is_ge, 9.0)
         op("v", lambda: g.vector.tensor_tensor_scan(T.cu[:, 16:80], T.odd[:], T.zz[:], 0.0, A.add, A.max), [R("odd"), R("zz")], [R("cu", 16, 80)])
-        mm(R("pE", 0, 1), [(T.pE[:, 0:1], T.mtri[:], T.cu[:, 79:80], True, True)], [R("cu", 16, 80), R("mtri")])
-        ts(R("cs", 15, 80), R("cu", 15, 80), A.add, R("pE", 0, 1), A.min, 256.0)
+        mm(R("pE", 384, 385), [(T.pE[:, 384:385], T.mtri[:], T.cu[:, 79:80], True, True)], [R("cu", 16, 80), R("mtri")])
+        run(gen, 1)
+        ts(R("cs", 15, 80), R("cu", 15, 80), A.add, R("pE", 384, 385), A.min, 256.0)
         tt(R("cv"), R("cs", 16, 80), R("cs", 15, 79), A.subtract)
         mm(R("pC", 256, 512), [(T.pC[:, 256 + 64 * j:320 + 64 * j], T.msel[:, 128 * j:128 * j + 128], T.cv[:], True, True) for j in four], [R("cv"), R("msel")])
+        run(gen, 1)
         cp(R("mp"), R("pC", 256, 512))
         dma("y", [(T.mt[0:128:16, :], T.mp[:])], [("mp", 0, 256)], [("mt", 0, 4096)])
-        spread(ET, ET, 512, 512, 1024)
+        spread(ET, ET, 0, 512, 1024)
+        run(gen)
+        if not last:
+            differences(t, 0, 2)
         ch = [0, 512, 1024, 1536]
         five("s", 0, 0, 1024)
         five("s", 0, 1024, 2048)
-        for c in range(2):
-            flag("s", 0, c)
-            flag("v", 1, c)
-        tt(R("ft"), R("ce"), R("pC", 0, 128), A.min)
-        ts(f1, R("pC", 0, 128), A.is_ge, BIG / 2)
-        ts(R("oe", 0, 128), R("ft"), A.add, R("lanef"))
+        if last:
+            break
+        for st in range(2):
+            for c in range(2):
+                flag(st, c, R(("pC", "pE")[st], 64 * c, 64 * c + 64))
+        first_list(R("pC", 0, 128), 0, 128)
+        ts(R("pC", 128, 256), R("pC", 0, 128), A.is_ge, BIG / 2)
+        for c in ch:
+            colour(0, c, c + 512)
+        step(0, 0, 512, R("B", R2, R2 + 512))
         tt(f2, f1, f2, A.mult)
-        if last:
-            for c in ch:
-                colour(0, c, c + 512)
-        else:
-            colour(0, 0, 1024)
-            colour(0, 1024, 2048)
-            place(t, 0)
-            n = at(t + 1, 0)
-            mm(R("pC", 256, 384), [(T.pC[:, 256:384], T.mper[:], n[0], True, True)], [n, R("mper")])
-            cp(R("wp"), R("pC", 256, 384))
-            dma("y", [(T.wt[16 * j:16 * j + 1, :], T.wp[64 * (j % 2):64 * (j % 2) + 64, :]) for j in range(8)], [("wp", 0, 128)], [("wt", 0, 8192)])
-        tt(R("ft"), R("zf"), f2, A.mult)
-        tt(R("ft"), R("ft"), R("sj"), A.add)
-        cp(R("oe", 128, 256), R("ft"))
-        if last:
-            tt(R("cc"), V(T.lq[:, 2], "lq"), f1, A.add)
-            tt(R("cc"), R("cc"), f2, A.add)
-            ts(R("cf"), R("cc"), A.min, 5.0)
-            send("r_yc", ("cf", 0, 128), lambda k: T.cf[:, 32 * order.index(k):32 * order.index(k) + 32], T.lc[me], ("lc", 0, 4), "l_end")
-            dma("y", [(T.yc[rows(me), 32 * o:32 * o + 32], T.cf[rows(o), 96:128]) for o in four], [("cf", 0, 128)], [])
-            dma("y", [(T.yc[rows(k), 32 * o:32 * o + 32], T.lc[k, rows(o), :]) for k in others for o in four], [("lc", 0, 4)], [])
-        base = (R1, S0)[t % 2]
+        place(t, 0)
+        n = at(t + 1, 0)
+        cp(R("wh", 0, 128), n)
+        tt(R("wh", 128, 256), n, R("wh", 0, 128), A.subtract)
+        mm(R("pD", 0, 512), [(T.pD[:, 128 * a:128 * a + 128], T.mw[:, 128 * a:128 * a + 128], T.wh[:, 128 * j:128 * j + 128], j == 0, j == 1) for a in four for j in range(2)],
+           [R("wh"), R("mw")])
+        second_list(f2, 0, 128)
+        cp(R("xg", 0, 512), R("pD", 0, 512))
+        dma("y", [(T.wt[0:128:16, :], T.xg[:, 0:512])], [("xg", 0, 512)], [("wt", 0, 8192)])
+        base = (R1, S0)[t]
 
         def second(c):
-            if not last:
-                step(1, c, c + 512, R("B", base + c, base + c + 512))
-                spread(base, 0, c, 512, 2048)
-                return
-            a = order[c // 512]
-            step(1, c, c + 512, R("eg", c, c + 512))
-            if a == me:
-                dma("s", [(T.yx[rows(me), 512 * o:512 * o + 512], T.eg[rows(o), c:c + 512]) for o in four], [("eg", c, c + 512)], [])
-                return
-            waits("g", "dma", [("eg", c, c + 512)], [])
-            es = eo if a in off else el
-            g.remote_dma_fused([transfer(a, es, "r_x%d" % me, T.eg[:, c:c + 512], T.ly[me])], local_sem=T.sem["l_end"])
-            nend[0] += len(es)
-            arrive(("ly", a, a + 1), "r_x%d" % a, len(es))
+            step(1, c, c + 512, R("B", base + c, base + c + 512))
+            for x0, x1 in SPREAD:
+                if x1 == c + 512:
+                    spread(base, 0, x0, x1 - x0, 2048)
 
-        gen = iter(()) if last else (x for a in range(2) for x in look("ss", t + 1, 0, a))
+        gen = (x for a in range(2) for x in look("ss", t + 1, 0, a))
         for j, c in enumerate(ch):
-            step(0, c, c + 512, R("B", R2 + c, R2 + c + 512))
-            five("s" if last or j < FIVE else "v", 1, c, c + 512)
+            if j:
+                step(0, c, c + 512, R("B", R2 + c, R2 + c + 512))
+            five("s" if j < FIVE else "v", 1, c, c + 512)
             colour(1, c, c + 512)
             if j:
                 second(ch[j - 1])
                 run(gen, 1)
         second(ch[3])
-        if not last:
-            run(gen)
-            run(look("sv", t + 1, 0, 2))
-            run(look("sv", t + 1, 0, 3))
-            for k in range(1, KEEP[t]):
-                place(t, k)
-            tt(R("cc"), R("cc"), f1, A.add)
-            tt(R("cc") if t == 0 else V(T.lz[:, 2], "lz", 2, 3), R("cc"), f2, A.add)
-            run(look("s", t + 1, 1, 0))
-            run(look("s", t + 1, 1, 1))
+        run(gen)
+        run(look("sv", t + 1, 0, 2))
+        run(look("sv", t + 1, 0, 3))
+        differences(t, 2, KEEP[t] + 1)
+        place(t, 1)
+        tt(R("cc"), R("cc"), R("pC", 128, 256), A.add)
+        tt(R("cc") if t == 0 else V(T.lz[:, 2], "lz", 2, 3), R("cc"), f2, A.add)
+        run(look("s", t + 1, 1, 0))
+        run(look("s", t + 1, 1, 1))
+        run(look("s", t + 1, 1, 2))
 
-    turn = lambda k: [j for j in four if far(j, k)].index(me) if far(k, me) else 2
-    for j, k in enumerate(sorted(others, key=turn)):
-        dma("y" if j == 0 else "ys", [(T.yx[rows(k), 512 * o:512 * o + 512], T.ly[k, rows(o), :]) for o in four], [("ly", k, k + 1)], [])
+    Y, G2 = (R("pC", 0, 64), R("pD", 0, 64)), (R("pE", 0, 64), R("pD", 512, 576))
+    for c in range(2):
+        flag(0, c, Y[c])
+        flag(1, c, G2[c])
+
+    def half(c):
+        first_list(Y[c], 64 * c, 64 * c + 64)
+        yield
+        tt(G2[c], R("f1", 64 * c, 64 * c + 64), G2[c], A.mult)
+        second_list(G2[c], 64 * c, 64 * c + 64)
+        yield
+
+    def cursors(c):
+        n = R("cc", 64 * c, 64 * c + 64)
+        tt(n, V(T.lq[:, 2, 2 * c:2 * c + 2], "lq"), R("f1", 64 * c, 64 * c + 64), A.add)
+        tt(n, n, G2[c], A.add)
+        for j in (2 * c, 2 * c + 1):
+            ts(R("xg", 544 * j + 512, 544 * j + 544), R("cc", 32 * j, 32 * j + 32), A.min, 5.0)
+
+    def store(q, k, src, need):
+        dma(q, [(T.yx[rows(k), 512 * o:512 * o + 512], src(o, 0, 512)) for o in four] + [(T.yc[rows(k), 32 * o:32 * o + 32], src(o, 512, 544)) for o in four], [need], [])
+
+    def leave(j):
+        a, c = order[j], 544 * j
+        step(1, 512 * j, 512 * j + 512, R("xg", c, c + 512))
+        if a == me:
+            store("s", me, lambda o, u, v: T.xg[rows(o), c + u:c + v], ("xg", c, c + 544))
+            return
+        waits("g", "dma", [("xg", c, c + 544)], [])
+        es = eo if a in off else el
+        g.remote_dma_fused([transfer(a, es, "r_x%d" % me, T.xg[:, c:c + 544], T.ly[me])], local_sem=T.sem["l_end"])
+        nend[0] += len(es)
+        arrive(("ly", a, a + 1), "r_x%d" % a, len(es))
+
+    h0, h1 = half(0), half(1)
+    run(h0, 1)
+    colour(0, 0, 512)
+    colour(0, 512, 1024)
+    step(0, 0, 512, R("B", R2, R2 + 512))
+    run(h0)
+    for j, c in enumerate(ch):
+        if j:
+            step(0, c, c + 512, R("B", R2 + c, R2 + c + 512))
+        five("s", 1, c, c + 512)
+        colour(1, c, c + 512)
+        if j == 0:
+            cursors(0)
+            run(h1)
+        if j < 2:
+            colour(0, c + 1024, c + 1536)
+        if j:
+            leave(j - 1)
+        if j == 2:
+            cursors(1)
+    leave(3)
+
+    for q, k in (("y", off[0]), ("ys", on[0]), ("ys", off[1])):
+        store(q, k, lambda o, u, v: T.ly[k, rows(o), u:v], ("ly", k, k + 1))
     for s in SENT:
         g.wait_ge(T.sem[s], SENT[s])
     g.wait_ge(T.sem["l_end"], nend[0])

from concourse.bass import DstId, RemoteDMATransfer
from concourse.mybir import AluOpType as A, ActivationFunctionType as F, AxisListType as X

TOP = 2 ** 20 - 1
BIG = 16384.0
SCRATCH = {}


def _buf(where, dtype, **shapes):
    for n, s in shapes.items():
        SCRATCH[n] = (where, s if isinstance(s, list) else [128, s], dtype)


S0, R1, ET, R2 = 0, 8192, 10240, 14336
_buf("dram", "int32", sr=[4, 128, 192], lr=[4, 128, 192])
_buf("dram", "float32", lp=[8, 128, 256], ly=[4, 128, 544])
_buf("sbuf", "int32", cq=[128, 36, 2, 32], xi=2048, la=768, xbt=1536, xbr=[128, 4, 6, 64], cxi=8, tho=1, zi=256, it0=144, it1=144, vci=96, pc=1, lane=1, grp=1, oi=1, ji=128, iq=128)
_buf("sbuf", "uint16", lw0=[128, 8, 96], lws=[128, 4, 12, 32], lwt=1536, lwr=[128, 4, 384], lx=768, ln=256, oe=256)
_buf("sbuf", "bfloat16", wr=6144, mt=4096, fl=1024, mcb=144, mid=128, mb2=144, vct=96, jh=128, cv=64, msel=512, mp=256, mw=512, wh=256)
_buf("sbuf", "float32", B=16384, wt=8192, xg=6144, eg=4096, es=[128, 8, 100], el=800, er=[128, 8, 100],
     colx=8, le=384, l1=192, l2=96, l3=32, lm=96, le2=384, thf=1, odd=64, zz=64, cu=80, cs=80,
     lb=512, lz=[128, 3, 4, 32], lq=[128, 3, 4, 32], dd=640, ce=128, zf=128, sj=128, f1=128, ft=128, fu=128, cc=128,
     lanef=1, grpf=1, of=1, k0=1, nk0=1, g16=1, nb=2, pb=2, cole=1, col1=1, isa=4, mtri=128)
_buf("psum", "float32", pA=2048, pD=1024, pC=512, pE=512)
PSUM = ("pA", "pD", "pC", "pE")
ENG = {"v": "q_v", "s": "q_s", "t": "q_t", "g": "q_g"}
DSEM = ["d%d" % j for j in range(100)]
SEMAPHORES = list(ENG.values()) + DSEM + ["r_p0", "r_p1", "r_q0", "r_q1", "r_e0", "r_e1", "r_ray", "r_lw", "r_xb", "r_x0", "r_x1", "r_x2", "r_x3",
                                          "r_f0", "r_f1", "r_f2", "l_px", "l_list", "l_end"]
FIVE = 2
FIRST = 0
INIT = "ssssss"
FS = 32
VX = (2, 4, 4)
SPREAD = ((0, 1024), (1024, 2048))
FOLD = (6, 7, 7)


def helper(core, T, topo):
    free = [c for c in topo.cores_of(core) if c not in T.cores and topo.die(c) == topo.die(core)]
    return free[0]


def mask(es):
    return sum(1 << e for e in es)


def rank_program(g, core, T, topo):
    me = T.rank_of(core)
    if me is None:
        for c in T.cores:
            if helper(c, T, topo) == core:
                rid, pid, _se = topo.addr(c)
                es = topo.engines(core, c)
                for t in range(3):
                    g.wait_ge(T.sem["r_f%d" % t], len(es))
                    g.remote_dma(T.B[:, R2 + 1024:R2 + 2048], T.xg[:, 1024 * t:1024 * t + 1024], T.sem["r_f%d" % t], T.sem["l_end"], pid, rid, mask(es))
                g.wait_ge(T.sem["l_end"], 3 * len(es))
        return
    Q = {"v": g.vector, "s": g.scalar, "t": g.tensor, "y": g.sync, "g": g}
    known = {q: {} for q in Q}
    snap = {}
    cnt = {q: 0 for q in ENG}
    hist = {}
    allsem = {}
    nd = [0]

    def wait(q, tok):
        sem, val = tok
        if known[q].get(sem, 0) >= val:
            return
        Q[q].wait_ge(T.sem[sem], val)
        known[q][sem] = val
        for s2, v2 in snap.get(tok, {}).items():
            known[q][s2] = max(known[q].get(s2, 0), v2)

    def waits(q, q0, reads, writes):
        toks = {}
        for wr, accs in ((False, reads), (True, writes)):
            for buf, lo, hi in accs:
                for (l, h, w, q2, tok) in hist.get(buf, ()):
                    same = q2 == q0 and q0 != "dma"
                    if buf in PSUM and not same:
                        hit = l // 512 <= (hi - 1) // 512 and lo // 512 <= (h - 1) // 512
                    else:
                        hit = l < hi and lo < h and (w or wr) and not (same and q0 == "t")
                    if hit:
                        toks[tok[0]] = max(toks.get(tok[0], 0), tok[1])
        for s in sorted(toks):
            wait(q, (s, toks[s]))

    def note(q, reads, writes, tok, apart=False):
        for buf, lo, hi in writes:
            hist[buf] = [e for e in hist.get(buf, ()) if apart or not (lo <= e[0] and e[1] <= hi)] + [(lo, hi, True, q, tok)]
        for buf, lo, hi in reads:
            hist[buf] = [e for e in hist.get(buf, ()) if not (lo <= e[0] and e[1] <= hi and not e[2] and e[3] == q and q in ENG)] + [(lo, hi, False, q, tok)]

    def R(n, a=0, b=None):
        b = SCRATCH[n][1][-1] if b is None else b
        return (T[n][:, a:b], [(n, a, b)])

    def V(ap, n, a=0, b=1 << 20):
        return (ap, [(n, a, b)])

    def ind(win, off):
        return (win[0].indirect(off[0]), win[1] + off[1])

    def op(q, fn, ins, outs):
        rd = [r for v in ins if isinstance(v, tuple) for r in v[1]]
        wr = [r for v in outs for r in v[1]]
        waits(q, q, rd, wr)
        i = fn()
        cnt[q] += 1
        i.then_inc(T.sem[ENG[q]], 1)
        tok = (ENG[q], cnt[q])
        allsem[ENG[q]] = cnt[q]
        snap[tok] = dict(known[q])
        note(q, rd, wr, tok)

    def dma(qs, items, ins, outs, apart=False):
        sem = DSEM[nd[0]]
        nd[0] += 1
        kn = {}
        for q in qs:
            waits(q, "dma", ins, [] if apart else outs)
            for s, v in known[q].items():
                kn[s] = max(kn.get(s, 0), v)
        for j, (o, i) in enumerate(items):
            Q[qs[j % len(qs)]].dma_start(o, i).then_inc(T.sem[sem], 16)
        tok = (sem, 16 * len(items))
        allsem[sem] = tok[1]
        snap[tok] = kn
        note("dma", ins, outs, tok, apart)

    sc_ = lambda v: v[0] if isinstance(v, tuple) else v

    def tt(o, a, b, f):
        op("v", lambda: g.vector.tensor_tensor(o[0], a[0], b[0], f), [a, b], [o])

    def ts(o, a, f, s, f2=None, s2=None):
        if f2 is None:
            op("v", lambda: g.vector.tensor_scalar(o[0], a[0], sc_(s), None, f), [a, s], [o])
        else:
            op("v", lambda: g.vector.tensor_scalar(o[0], a[0], sc_(s), sc_(s2), f, f2), [a, s, s2], [o])

    def cp(o, a):
        op("v", lambda: g.vector.tensor_copy(o[0], a[0]), [a], [o])

    def act(o, a, bias=0.0, scale=1.0):
        op("s", lambda: g.scalar.activation(o[0], a[0], F.Identity, bias=sc_(bias), scale=scale), [a, bias], [o])

    def fill(o, c):
        op("v", lambda: g.vector.memset(o[0], c), [], [o])

    def mm(o, calls, ins):
        def fn():
            last = None
            for c in calls:
                last = g.tensor.matmul(*c)
            return last
        op("t", fn, ins, [o])

    def run(gen, n=99):
        for _ in range(n):
            next(gen, None)

    others = [k for k in range(4) if k != me]
    far = lambda a, b: topo.chip(T.cores[a]) != topo.chip(T.cores[b])
    away = lambda a: sorted((k for k in range(4) if far(k, a)), key=lambda k: topo.die(T.cores[k]) != topo.die(T.cores[a]))
    off = away(me)
    on = [k for k in others if k not in off]
    eo = topo.engines(core, T.cores[off[0]])
    el = [e for e in topo.engines(core, T.cores[on[0]]) if e not in eo]
    eng = {}
    for ks, es in ((off, eo), (on, el)):
        n = len(es) // len(ks)
        for j, k in enumerate(ks):
            eng[k] = es[j * n:j * n + n]
    ARR = len(eo) + len(el)
    SENT = {"l_px": 2 * ARR, "l_list": 5 * ARR}
    nend = [0]

    def transfer(k, es, sem, src, dst):
        rid, pid, _se = topo.addr(T.cores[k])
        return RemoteDMATransfer(dst_ids=[DstId(rid=rid, pnc=pid)], dma_engine_mask=mask(es), remote_sem=T.sem[sem], src=src, dst=dst)

    def send(sem, need, src, dst, land, loc):
        waits("g", "dma", [need], [])
        g.remote_dma_fused([transfer(k, eng[k], sem, src(k), dst) for k in others], local_sem=T.sem[loc])
        if loc in SENT:
            hist[need[0]].append((need[1], need[2], False, "remote", (loc, SENT[loc])))
        else:
            nend[0] += ARR
        arrive(land, sem, ARR)

    def arrive(land, sem, n):
        allsem[sem] = n
        hist.setdefault(land[0], []).append((land[1], land[2], True, "remote", (sem, n)))

    rows = lambda o: slice(32 * o, 32 * o + 32)
    order = off + on + [me]
    four = range(4)

    dma("s", [(T.zi[:, 0:128], T.ray[:, 0:128])], [], [("zi", 0, 128)])
    dma("s", [(T.cq[:, 0:12], T.cand[:, 0:768])], [], [("cq", 0, 768)])
    for hf in range(2):
        dma("y", [(T.xi[:, 1024 * hf + 256 * k:1024 * hf + 256 * k + 256], T.px[rows(k), 1024 * hf:1024 * hf + 1024]) for k in order],
            [], [("xi", 1024 * hf, 1024 * hf + 1024)])
    dma("s", [(T.tho[:], T.th[:])], [], [("tho", 0, 1)])
    for n, a, b, pat, base, cm in [("pc", 0, 1, [[0, 1]], 0, 1), ("it1", 0, 143, [[1, 143]], -15, -1), ("vci", 0, 96, [[0, 3], [16, 32]], -255, 0),
                                   ("it0", 0, 143, [[1, 143]], 0, 0), ("ji", 0, 128, [[16, 128]], 0, 0)] + [
                                   ("iq", 32 * o, 32 * o + 32, [[16, 2], [32, 4], [4, 4]], 0, -1) for o in four]:
        op("g", lambda: g.iota(T[n][:, a:b], pat, base, cm), [], [R(n, a, b)])
    fill(R("wt", 0, 2048), 0.0)
    ts(R("lane"), R("pc"), A.bitwise_and, 15)
    fill(V(T.es[:, :, 96:100], "es"), 0.0)
    cp(R("lanef"), R("lane"))
    ts(R("k0"), R("lane"), A.is_equal, 0)
    cp(R("lb", 0, 128), R("zi", 0, 128))
    dma("y", [(T.wt[0:128:16, 0:2048], T.lb[:, 0:128])], [("lb", 0, 128)], [("wt", 0, 2048)])
    dma("y", [(T.cq[:, 12:36], T.cand[:, 768:2304])], [], [("cq", 768, 2304)])
    ts(R("nk0"), R("k0"), A.mult, -BIG)

    def pixels(hf):
        c = 2048 + 1024 * hf
        cp(R("eg", c, c + 1024), R("xi", c - 2048, c - 1024))
        waits("g", "dma", [("eg", c, c + 1024)], [])
        sem = lambda k: ("r_p%d" if k in off else "r_q%d") % hf
        g.remote_dma_fused([transfer(k, eng[k], sem(k), T.eg[:, c + 256 * k:c + 256 * k + 256], T.lp[4 * hf + me]) for k in others], local_sem=T.sem["l_px"])
        hist["eg"].append((c, c + 1024, False, "remote", ("l_px", SENT["l_px"])))
        for k in others:
            arrive(("lp", 4 * hf + k, 4 * hf + k + 1), sem(k), len(eo) if k in off else len(el))

    def table_x(q, hf, who):
        c = 1024 * hf
        src = lambda a: T.eg[:, 2048 + c + 256 * a:2048 + c + 256 * a + 256] if a == me else T.lp[4 * hf + a]
        col = lambda a, o: 2048 + 2048 * ((a - o - 1) % 4) + c
        dma(q, [(T.B[rows(o), col(a, o):col(a, o) + 1024], src(a)) for a in who for o in four],
            [("eg", 2048 + c, 3072 + c) if a == me else ("lp", 4 * hf + a, 4 * hf + a + 1) for a in who], [("B", 2048 * d + c, 2048 * d + c + 1024) for d in (1, 2, 3, 4)], apart=True)

    def places(c, n, outs, lane, add):
        p = R("pA", 1024, 1024 + n)
        ts(R("xi", 0, n), c, A.bitwise_and, 15)
        ts(p, R("xi", 0, n), A.mult, 16.0 * lane - 1)
        tt(p, c, p, A.add)
        for m in range(3):
            ts(outs(m), R("pA", 1024 + m * n // 3, 1024 + (m + 1) * n // 3), A.mult, 0.0625, A.add, add)

    def prep0(h):
        places(V(T.cq[:, 0:12, h, :], "cq", 0, 768), 384, lambda m: V(T.lw0[:, 4 * h:4 * h + 4, 32 * m:32 * m + 32], "lw0", h, h + 1), 128, 0.0)

    def prep(t):
        places(V(T.cq[:, 12 * t:12 * t + 12], "cq", 768 * t, 768 * t + 768), 768, lambda m: V(T.lws[:, :, 6 * t - 6 + m:6 * t:3, :], "lws"), 512, 128.0 * me)

    nw = [0]

    def look_w(qs, win, lst, nbias, pbias, out):
        c, n = 1536 * (nw[0] % 4), 96 // len(qs)
        nw[0] += 1
        for j, q in enumerate(qs):
            o, src = R("wr", c + 16 * n * j, c + 16 * n * (j + 1)), ind(win, lst(n * j, n * (j + 1)))
            if q == "s":
                act(o, src, bias=nbias)
            else:
                ts(o, src, A.subtract, pbias)
            if j == len(qs) - 1:
                mm(out, [(out[0], T.mid[:], T.vct[:], True, False)] + [(out[0], T.mcb[:, 15 - i:143 - i], T.wr[:, c + i:c + 1536:16], False, i == 15) for i in range(16)],
                   [R("mid"), R("vct"), R("mcb"), R("wr", c, c + 1536)])
            yield

    def look0(qs, h, o):
        b = 1024.0 * o + 512.0 * h + 255.0
        run(look_w(qs, R("wt", 0, 2048), lambda u, v: V(T.lw0[:, 4 * h + o, u:v], "lw0", h, h + 1), -b, b, R(("pA", "pE")[h], 96 * o, 96 * o + 96)))

    def seen0(h, qs):
        for o in four:
            p = R(("pA", "pE")[h], 96 * o, 96 * o + 96)
            ts(p, p, A.max, 0.0, A.subtract, 2048.0 * ((me - o - 1) % 4))
        for o in four:
            c = 400 * h + 100 * o
            tt(V(T.es[:, 4 * h + o, 0:96], "es", c, c + 96), V(T.cq[:, o:12:4, h, :], "cq", 0, 768), R(("pA", "pE")[h], 96 * o, 96 * o + 96), A.subtract)
        c = 400 * h
        dma(qs, [(T.el[rows(o), c + 100 * k:c + 100 * k + 100], T.es[rows(k), 4 * h + o, :]) for k in others for o in four], [("es", c, c + 400)], [("el", c, c + 400)])
        send("r_e%d" % h, ("el", c, c + 400), lambda k: T.el[:, c + 100 * k:c + 100 * k + 100], T.er[:, 4 * h + me, :], ("er", c, c + 400), "l_list")

    def seen_own(h):
        c = 400 * h
        dma("y", [(T.er[rows(o), 4 * h + me, :], T.es[rows(me), 4 * h + o, :]) for o in four], [("es", c, c + 400)], [("er", c, c + 400)], apart=True)

    def consts():
        ts(R("grp"), R("pc"), A.arith_shift_right, 4)
        ts(R("zi", 0, 128), R("it0", 0, 128), A.arith_shift_right, 4)
        ts(R("oi"), R("pc"), A.arith_shift_right, 5)
        cp(R("grpf"), R("grp"))
        cp(R("of"), R("oi"))
        ts(R("g16"), R("grpf"), A.mult, 16.0, A.add, 15.0)
        for h in range(2):
            ts(R("nb", h, h + 1), R("of"), A.mult, -1024.0, A.add, -(512.0 * h + 255.0))
            ts(R("pb", h, h + 1), R("of"), A.mult, 1024.0, A.add, 512.0 * h + 255.0)
        ts(R("cole"), R("of"), A.mult, -1024.0, A.add, 4096.0)
        ts(R("cxi", 0, 4), R("it0", 3, 7), A.subtract, R("of"))
        ts(R("cxi", 4, 8), R("it0", 4, 8), A.subtract, R("of"))
        ts(R("cxi"), R("cxi"), A.bitwise_and, 3)
        ts(R("colx"), R("cxi"), A.mult, 2048.0)
        ts(R("col1"), R("lanef"), A.mult, -1.0, A.add, 2048.0)
        ts(R("mb2", 0, 143), R("it0", 0, 143), A.subtract, R("g16"), A.is_equal, 0.0)
        ts(R("fu"), R("it1", 15, 143), A.is_gt, 0)
        ts(R("f1"), R("zi", 0, 128), A.is_equal, R("grpf"))
        cp(R("jh"), R("ji"))
        ts(R("sj"), R("ji"), A.add, R("lanef"), A.add, 4096.0)
        tt(R("mtri"), R("f1"), R("fu"), A.mult)
        yield
        ts(R("zi", 128, 256), R("it1", 15, 143), A.bitwise_and, 31)
        for j in four:
            ts(R("isa", j, j + 1), R("of"), A.is_equal, float(j))
        for j in four:
            ts(R("mw", 128 * j, 128 * j + 128), R("zi", 128, 256), A.is_equal, 0, A.mult, R("isa", j, j + 1))
            ts(R("msel", 128 * j, 128 * j + 128), R("iq"), A.is_equal, -j)
        fill(R("zz"), 0.0)
        fill(R("cu", 0, 16), 0.0)
        fill(R("cc"), 0.0)

    def later(src, need, tn, ln, sem):
        til, lan = T[tn], T[ln]
        dma("y", [(lan[rows(o), k] if k == me else til[rows(o), 384 * k:384 * k + 384], src(k, o)) for k in order for o in four], [need], [(tn, 0, 1536), (ln, 0, 1536)])
        send(sem, (tn, 0, 1536), lambda k: til[:, 384 * k:384 * k + 384], lan[:, me], (ln, 0, 1536), "l_list")

    pixels(0)
    ts(R("mcb", 0, 143), R("it1", 0, 143), A.is_equal, 0, A.mult, R("nk0"))
    prep0(0)
    ts(R("mid"), R("it1", 15, 143), A.is_equal, 0)
    ts(R("vct"), R("vci"), A.add, R("lanef"), A.mult, BIG)
    look0("s", 0, 0)
    pixels(1)
    table_x("y", 0, [me])
    table_x("y", 1, [me])
    cp(V(T.es[:, me, 96:97], "es", 100 * me + 96, 100 * me + 97), R("tho"))
    look0("s", 0, 1)
    look0("v", 0, 3)
    prep0(1)
    look0("s", 0, 2)
    look0("s", 1, 0)
    table_x("y", 0, on)
    table_x("y", 1, on)
    gen = consts()
    run(gen, 1)
    seen0(0, "y")
    run(gen)
    seen_own(0)
    table_x("y", 0, off)
    table_x("y", 1, off)
    look0("s", 1, 1)
    look0("s", 1, 2)
    look0("s", 1, 3)
    prep(1)
    dma("y", [(T.sr[:], T.ray[:])], [], [("sr", 0, 4)])

    def look(qs, t, h, a):
        c = 192 * (t - 1) + 96 * h
        return look_w(qs, R("wt"), lambda u, v: V(T.lwr[:, a, c + u:c + v], "lwr"), R("nb", h, h + 1), R("pb", h, h + 1), R("pD", 512 * h + 96 * a, 512 * h + 96 * a + 96))

    def lists(t, h):
        p = R("pD", 512 * h, 512 * h + 384)
        if t == 0:
            E = lambda a, b: V(T.er[:, 4 * h + a:4 * h + b, 0:96], "er", 400 * h, 400 * h + 400)
            ts(p, E(0, 4), A.mult, -1.0)
        else:
            E = lambda a, b: R("le", 96 * a, 96 * b)
            for a in four:
                q = R("pD", 512 * h + 96 * a, 512 * h + 96 * a + 96)
                ts(q, q, A.max, 0.0, A.subtract, R("colx", 4 * t - 4 + a, 4 * t - 3 + a))
            tt(E(0, 4), V(T.xbr[:, :, 3 * t - 3:3 * t, 32 * h:32 * h + 32], "xbr"), p, A.subtract)
        tt(R("l1"), E(0, 2), E(2, 4), A.max)
        tt(R("l2"), R("l1", 0, 96), R("l1", 96, 192), A.max)
        tt(R("l3"), R("l2", 0, 32), R("l2", 32, 64), A.max)
        for m in range(3):
            tt(R("lm", 32 * m, 32 * m + 32), R("l3"), R("l2", 64, 96), A.max)
        for a in four:
            q = R("pD", 512 * h + 96 * a, 512 * h + 96 * a + 96)
            tt(q, q, R("lm"), A.min)
        tt(R("le2"), E(0, 4), p, A.max)
        cp(R("lx", 384 * h, 384 * h + 384), R("le2"))

    def acc(h):
        return R("pA", 1024 * h, 1024 * h + 512), R("pA", 1024 * h + 512, 1024 * h + 1024)

    first = lambda t, h: 0 if h else FOLD[t]

    def pix(t, h, k, n):
        return R("eg" if k < first(t, h) else "xg", 512 * k, 512 * n)

    def gather_x(q, t, h, k, n):
        w = 0 if t == 2 else 2048
        src = ind(R("B", w, w + 8192), R("lx", 384 * h + 32 * k, 384 * h + 32 * n))
        if q == "v":
            cp(pix(t, h, k, n), src)
        else:
            act(pix(t, h, k, n), src)
        if k == first(t, h):
            if "v" != INIT[2 * t + h]:
                act(acc(h)[1], pix(t, h, k, k + 1))

    def minmax(t, h, k0, n):
        lo, hi = acc(h)
        for k in range(max(k0, first(t, h) + 1), n):
            x = pix(t, h, k, k + 1)
            if k == first(t, h) + 1 and "v" == INIT[2 * t + h]:
                cp(hi, pix(t, h, k - 1, k))
            tt(R("B", ET + 512, ET + 1024) if (h, k) == (1, 11) else lo, x, hi if k == first(t, h) + 1 else lo, A.min)
            tt(hi, x, hi, A.max)

    def fold(t):
        c = helper(core, T, topo)
        rid, pid, _se = topo.addr(c)
        es = topo.engines(core, c)
        n = len(es) // 2
        srcs = [pix(t, 0, k, k + 1) for k in range(FOLD[t])]
        waits("g", "dma", [v[1][0] for v in srcs], [("B", R2 + 1024, R2 + 2048)])
        g.remote_dma_fused([RemoteDMATransfer(dst_ids=[DstId(rid=rid, pnc=pid)], dma_engine_mask=mask(es[j * n:j * n + n]), remote_sem=T.sem["r_f%d" % t],
                                              srcs=[v[0] for v in srcs],
                                              dsts=[T.xg[:, 1024 * t + 512 * j:1024 * t + 512 * j + 512]], alu_op=(3, 2)[j]) for j in range(2)], local_sem=T.sem["l_end"])
        nend[0] += 2 * n
        back = len(topo.engines(c, core))
        for v in srcs:
            hist[v[1][0][0]].append(v[1][0][1:] + (False, "remote", ("r_f%d" % t, back)))
        arrive(("B", R2 + 1024, R2 + 2048), "r_f%d" % t, back)

    def merge():
        lo, hi = acc(0)
        tt(R("B", ET, ET + 512), R("B", R2 + 1024, R2 + 1536), lo, A.min)
        tt(hi, R("B", R2 + 1536, R2 + 2048), hi, A.max)

    def flags(h):
        c = 512 * h
        lt, fl = R("B", R2 + c, R2 + c + 512), R("fl", c, c + 512)
        act(lt, R("B", ET + c, ET + c + 512), bias=R("thf"))
        tt(fl, acc(h)[1], lt, A.is_gt)
        mm(R("pC", 0, 64), [(T.pC[:, 0:64], T.mb2[:, 15 - i:143 - i], T.fl[:, 64 * i:64 * i + 64], i == 8, i == 7) for i in range(8 * h, 8 * h + 8)], [fl, R("mb2")])

    def spread(src, dst, lo, w, width):
        items = []
        for d in (1, 2, 3):
            c, k = dst + d * width + lo, 32 * (4 - d)
            items.append((T.B[0:k, c:c + w], T.B[32 * d:128, src + lo:src + lo + w]))
            items.append((T.B[k:128, c:c + w], T.B[0:32 * d, src + lo:src + lo + w]))
        dma("y", items, [("B", src + lo, src + lo + w)], [("B", dst + d * width + lo, dst + d * width + lo + w) for d in (1, 2, 3)])

    def at(t, k, n=1):
        if t < 2:
            return R(("la", "lb")[t], 128 * k, 128 * (k + n))
        return V(T.lz[:, k:k + n], "lz", k, k + n)

    def place_lists(src):
        yield cp(R("ln"), src)
        yield ts(R("zi"), src, A.add, R("cole"))
        yield ts(R("zi"), R("zi"), A.bitwise_and, 4095)
        yield ts(R("ce"), R("zi", 0, 128), A.add, R("col1"))
        yield tt(R("zf"), R("zi", 128, 256), R("sj"), A.subtract)

    f1, f2 = R("f1"), R("pE", 0, 128)

    def place(t, k):
        c = 128 * k
        tt(R("pE", 128, 256), R("dd", c, c + 128), R("pC", 128, 256), A.mult)
        tt(R("fu"), R("dd", c + 128, c + 256), f2, A.mult)
        tt(R("pE", 128, 256), at(t, k), R("pE", 128, 256), A.add)
        tt(at(t + 1, k), R("fu"), R("pE", 128, 256), A.add)

    def first_list(y, a, b):
        tt(R("ft", a, b), R("ce", a, b), y, A.min)
        ts(R("oe", a, b), R("ft", a, b), A.add, R("lanef"))
        ts(R("f1", a, b), y, A.is_ge, BIG / 2)

    def second_list(f, a, b):
        tt(R("pE", 256 + a, 256 + b), R("zf", a, b), f, A.mult)
        tt(R("ft", a, b), R("sj", a, b), R("pE", 256 + a, 256 + b), A.add)
        cp(R("oe", 128 + a, 128 + b), R("ft", a, b))

    def flag(st, c, o):
        b, l0 = 2048 * st + 1024 * c, 128 * st + 64 * c
        w, sc = R("wr", b, b + 1024), (-1.0, -1.0 / BIG)[st]
        act(R("wr", b, b + 16 * FS), ind(R("mt"), R("ln", l0, l0 + FS)), scale=sc)
        if FS < 64:
            ts(R("wr", b + 16 * FS, b + 1024), ind(R("mt"), R("ln", l0 + FS, l0 + 64)), A.mult, sc)
        mm(o, [(o[0], T.mid[:], T.jh[:, 64 * c:64 * c + 64], True, False)] * (1 - st) +
           [(o[0], T.mcb[:, 15 - i:143 - i], T.wr[:, b + i:b + 1024:16], st == 1 and i == 0, i == 15) for i in range(16)], [w, R("mcb"), R("mid"), R("jh")])

    def colour(st, x0, x1):
        b = 2048 * st
        win = R("B", ET, R2 + x1) if st else R("B", R1, R2)
        act(R("eg", b + x0, b + x1), ind(win, R("oe", (b + x0) // 16, (b + x1) // 16)), bias=-0.375, scale=-0.25)

    def five(q, st, x0, x1):
        x, z = R("B", (R1, R2)[st] + x0, (R1, R2)[st] + x1), R("pA", x0, x1)
        if q == "s":
            act(z, x, scale=1.25)
        else:
            ts(z, x, A.mult, 1.25)

    def step(st, x0, x1, out):
        y = R("xi", x0, x1)
        tt(y, R("eg", 2048 * st + x0, 2048 * st + x1), R("pA", x0, x1), A.add)
        ts(out, y, A.max, 0.0, A.min, float(TOP))

    KEEP = (4, 2, 0)

    def differences(t, a, b):
        n = ("la", "lb")[t]
        tt(R("dd", 128 * a, 128 * b), R(n, 128 * a + 128, 128 * b + 128), R(n, 128 * a, 128 * b), A.subtract)

    def regroup():
        dma("y", [(T.lq[rows(o), :, j, :], T.lz[rows(a), :, o, :]) for o in four for j, a in enumerate(order)], [("lz", 0, 3)], [("lq", 0, 1 << 20)])
        dma("y", [(T.B[rows(o), R1 + 512 * j:R1 + 512 * j + 512], T.B[rows(a), 512 * o:512 * o + 512]) for o in four for j, a in enumerate(order)],
            [("B", 0, 2048)], [("B", R1, R1 + 2048)])

    for t in range(3):
        last = t == 2
        lists(t, 0)
        n = FOLD[t]
        if t == 0:
            seen0(1, "y")
            seen_own(1)
            prep(2)
        if t:
            run(look("v", t, 1, 3))
        gather_x("s", t, 0, 0, n - VX[t])
        if VX[t]:
            gather_x("v", t, 0, n - VX[t], n)
        fold(t)
        if last:
            regroup()
        if t == 0:
            send("r_ray", ("sr", 0, 4), lambda k: T.sr[k], T.lr[me], ("lr", 0, 4), "l_list")
            op("g", lambda: g.iota(T.mt[:], [[0, 4096]], 0, 0, allow_small_or_imprecise_dtypes=True), [], [R("mt")])
        for k0, k1 in ((n, n + 1), (n + 1, n + 2), (n + 2, 9), (9, 12)) if n < 7 else ((n, n + 1), (n + 1, n + 2), (n + 2, 12)):
            gather_x("s", t, 0, k0, k1)
        if t == 0:
            waits("y", "dma", pix(t, 0, n + 1, n + 2)[1], [])
            later(lambda k, o: T.lws[rows(k), o], ("lws", 0, 1 << 20), "lwt", "lwr", "r_lw")
            later(lambda k, o: T.cq[rows(k), 12 + o:36:4], ("cq", 768, 2304), "xbt", "xbr", "r_xb")
            op("g", lambda: g.iota(T.wt[:, 6144:8192], [[0, 2048]], 0, 0, allow_small_or_imprecise_dtypes=True), [], [R("wt", 6144, 8192)])
        if t == 0:
            minmax(t, 0, n, n + FIRST)
        lists(t, 1)
        if t == 1:
            place(0, 2)
            minmax(t, 0, n, n + 2)
            place(0, 3)
        minmax(t, 0, n + (FIRST, 2, 0)[t], 12)
        if t == 0:
            dma("y", [(T.la[rows(a), :], T.ray[rows(me), :] if a == me else T.lr[a]) for a in four], [("lr", 0, 4)], [("la", 0, 768)])
            op("v", lambda: g.vector.tensor_reduce(T.thf[:], T.er[:, 0:4, 96], X.X, A.add), [V(None, "er", 0, 400)], [R("thf")])
        for k0, k1 in ((0, 1), (1, 3), (3, 6), (6, 9), (9, 10), (10, 11), (11, 12)):
            gather_x("s", t, 1, k0, k1)
        for c in (2048, 4096) if t == 0 else ():
            act(R("wt", c, c + 2048), R("wt", 0, 2048))
        minmax(t, 1, 0, 12)
        spread(ET, ET, 512, 512, 1024)
        flags(1)
        merge()
        flags(0)
        gen = place_lists(V(T.lq[:, 0:2], "lq") if last else at(t, 0, 2))
        run(gen, 2)
        ts(R("odd"), R("pC", 0, 64), A.is_ge, 9.0)
        op("v", lambda: g.vector.tensor_tensor_scan(T.cu[:, 16:80], T.odd[:], T.zz[:], 0.0, A.add, A.max), [R("odd"), R("zz")], [R("cu", 16, 80)])
        mm(R("pE", 384, 385), [(T.pE[:, 384:385], T.mtri[:], T.cu[:, 79:80], True, True)], [R("cu", 16, 80), R("mtri")])
        run(gen, 1)
        ts(R("cs", 15, 80), R("cu", 15, 80), A.add, R("pE", 384, 385), A.min, 256.0)
        tt(R("cv"), R("cs", 16, 80), R("cs", 15, 79), A.subtract)
        mm(R("pC", 256, 512), [(T.pC[:, 256 + 64 * j:320 + 64 * j], T.msel[:, 128 * j:128 * j + 128], T.cv[:], True, True) for j in four], [R("cv"), R("msel")])
        run(gen, 1)
        cp(R("mp"), R("pC", 256, 512))
        dma("y", [(T.mt[0:128:16, :], T.mp[:])], [("mp", 0, 256)], [("mt", 0, 4096)])
        spread(ET, ET, 0, 512, 1024)
        run(gen)
        if not last:
            differences(t, 0, 2)
        ch = [0, 512, 1024, 1536]
        five("s", 0, 0, 1024)
        five("s", 0, 1024, 2048)
        if last:
            break
        for st in range(2):
            for c in range(2):
                flag(st, c, R(("pC", "pE")[st], 64 * c, 64 * c + 64))
        first_list(R("pC", 0, 128), 0, 128)
        ts(R("pC", 128, 256), R("pC", 0, 128), A.is_ge, BIG / 2)
        for c in ch:
            colour(0, c, c + 512)
        step(0, 0, 512, R("B", R2, R2 + 512))
        tt(f2, f1, f2, A.mult)
        place(t, 0)
        n = at(t + 1, 0)
        cp(R("wh", 0, 128), n)
        tt(R("wh", 128, 256), n, R("wh", 0, 128), A.subtract)
        mm(R("pD", 0, 512), [(T.pD[:, 128 * a:128 * a + 128], T.mw[:, 128 * a:128 * a + 128], T.wh[:, 128 * j:128 * j + 128], j == 0, j == 1) for a in four for j in range(2)],
           [R("wh"), R("mw")])
        second_list(f2, 0, 128)
        cp(R("xg", 0, 512), R("pD", 0, 512))
        dma("y", [(T.wt[0:128:16, :], T.xg[:, 0:512])], [("xg", 0, 512)], [("wt", 0, 8192)])
        base = (R1, S0)[t]

        def second(c):
            step(1, c, c + 512, R("B", base + c, base + c + 512))
            for x0, x1 in SPREAD:
                if x1 == c + 512:
                    spread(base, 0, x0, x1 - x0, 2048)

        gen = (x for a in range(2) for x in look("ss", t + 1, 0, a))
        for j, c in enumerate(ch):
            if j:
                step(0, c, c + 512, R("B", R2 + c, R2 + c + 512))
            five("s" if j < FIVE else "v", 1, c, c + 512)
            colour(1, c, c + 512)
            if j:
                second(ch[j - 1])
                run(gen, 1)
        second(ch[3])
        run(gen)
        run(look("sv", t + 1, 0, 2))
        run(look("sv", t + 1, 0, 3))
        differences(t, 2, KEEP[t] + 1)
        place(t, 1)
        tt(R("cc"), R("cc"), R("pC", 128, 256), A.add)
        tt(R("cc") if t == 0 else V(T.lz[:, 2], "lz", 2, 3), R("cc"), f2, A.add)
        run(look("s", t + 1, 1, 0))
        run(look("s", t + 1, 1, 1))
        run(look("s", t + 1, 1, 2))

    Y, G2 = (R("pC", 0, 64), R("pD", 0, 64)), (R("pE", 0, 64), R("pD", 512, 576))
    for c in range(2):
        flag(0, c, Y[c])
        flag(1, c, G2[c])

    def half(c):
        first_list(Y[c], 64 * c, 64 * c + 64)
        yield
        tt(G2[c], R("f1", 64 * c, 64 * c + 64), G2[c], A.mult)
        second_list(G2[c], 64 * c, 64 * c + 64)
        yield

    def cursors(c):
        n = R("cc", 64 * c, 64 * c + 64)
        tt(n, V(T.lq[:, 2, 2 * c:2 * c + 2], "lq"), R("f1", 64 * c, 64 * c + 64), A.add)
        tt(n, n, G2[c], A.add)
        for j in (2 * c, 2 * c + 1):
            ts(R("xg", 544 * j + 512, 544 * j + 544), R("cc", 32 * j, 32 * j + 32), A.min, 5.0)

    def store(q, k, src, need):
        dma(q, [(T.yx[rows(k), 512 * o:512 * o + 512], src(o, 0, 512)) for o in four] + [(T.yc[rows(k), 32 * o:32 * o + 32], src(o, 512, 544)) for o in four], [need], [])

    def leave(j):
        a, c = order[j], 544 * j
        step(1, 512 * j, 512 * j + 512, R("xg", c, c + 512))
        if a == me:
            store("s", me, lambda o, u, v: T.xg[rows(o), c + u:c + v], ("xg", c, c + 544))
            return
        waits("g", "dma", [("xg", c, c + 544)], [])
        es = eo if a in off else el
        g.remote_dma_fused([transfer(a, es, "r_x%d" % me, T.xg[:, c:c + 544], T.ly[me])], local_sem=T.sem["l_end"])
        nend[0] += len(es)
        arrive(("ly", a, a + 1), "r_x%d" % a, len(es))

    h0, h1 = half(0), half(1)
    run(h0, 1)
    colour(0, 0, 512)
    colour(0, 512, 1024)
    step(0, 0, 512, R("B", R2, R2 + 512))
    run(h0)
    for j, c in enumerate(ch):
        if j:
            step(0, c, c + 512, R("B", R2 + c, R2 + c + 512))
        five("s", 1, c, c + 512)
        colour(1, c, c + 512)
        if j == 0:
            cursors(0)
            run(h1)
        if j < 2:
            colour(0, c + 1024, c + 1536)
        if j:
            leave(j - 1)
        if j == 2:
            cursors(1)
    leave(3)

    for q, k in (("y", off[0]), ("ys", on[0]), ("ys", off[1])):
        store(q, k, lambda o, u, v: T.ly[k, rows(o), u:v], ("ly", k, k + 1))
    for s in SENT:
        g.wait_ge(T.sem[s], SENT[s])
    g.wait_ge(T.sem["l_end"], nend[0])
    for s in sorted(allsem):
        wait("y", (s, allsem[s]))
